import numpy as np, ml_dtypes
CORES = [2,6,10,14,18,22,26,30]
N = 8
import mx_ref
BF = ml_dtypes.bfloat16
def gcols(t, e):
    v = np.concatenate([t.reshape(8, 16, -1, 4), np.zeros((8, 16, 1, 4), BF)], axis=2)
    return np.ascontiguousarray(np.stack([v[g][:, e[g]] for g in range(8)])).reshape(128, -1)
def tile(rs):
    return np.stack(rs, axis=2).reshape(128, -1).astype(BF)
def cut(t, i, w=512):
    return t[:, w * i:w * i + w]
def pick(q, e):
    c = np.concatenate([q[0].reshape(128, -1, 4), np.zeros((128, 1, 4), np.uint8)], axis=1); s = np.concatenate([q[1], np.ones((16, 1), np.uint8)], axis=1)
    return (np.ascontiguousarray(c[:, e].reshape(128, -1)), np.ascontiguousarray(s[:, e]))
def join(*qs):
    return (np.concatenate([q[0] for q in qs], axis=1), np.concatenate([q[1] for q in qs], axis=1))
def put(q, e, v):
    c, s = q[0].reshape(128, -1, 4).copy(), q[1].copy(); c[:, e] = v[0].reshape(128, -1, 4); s[:, e] = v[1]
    return (c.reshape(128, -1), s)
def pk(c, s):
    return (np.ascontiguousarray(c), mx_ref.live(s))
def emit(q):
    return q[0], q[1]
def packed(v, rng):
    q = [mx_ref.quantize(np.ascontiguousarray(v[r])) for r in range(N)]
    return np.stack([a for a, b in q]), np.stack([mx_ref.plane(b, rng) for a, b in q])
def values_of_codes():
    e, c = np.zeros((128, 128, 4), np.float32), np.zeros((128, 2, 4), np.uint8)
    e[np.arange(128), np.arange(128), 0] = 1
    c[:127, :, 0] = np.arange(256).reshape(2, 128).T[:127]
    return mx_ref.matmul(mx_ref.quantize(e.reshape(128, 512).astype(BF)), (c.reshape(128, 8), np.full((16, 2), 127, np.uint8))).T.reshape(-1).astype(np.float64)
CODE_VALUE, SCALE_VALUE = values_of_codes(), 2.0 ** (np.arange(256) - 127.0)
def decode(q):
    return (CODE_VALUE[q[0]].reshape(16, 8, -1, 4) * SCALE_VALUE[q[1]][:, None, :, None] + 0.0).reshape(128, -1).astype(np.float32)
def f(rng, *shape):
    return mx_ref.flush((rng.standard_normal(shape, dtype=np.float32) * np.exp2(rng.integers(-2, 3, shape[:-1] + (1,)))).astype(BF))
def wide(rng, *shape, cols=0):
    v = rng.standard_normal(shape, dtype=np.float32) * np.exp2(rng.integers(-12, 13, shape)).astype(np.float32)
    if cols: v *= np.repeat(np.exp2(rng.integers(-cols, cols + 1, shape[:-2] + (1, shape[-1] // 4))) * (rng.random(shape[:-2] + (1, shape[-1] // 4)) > 0.0625), 4, axis=-1).astype(np.float32)
    return mx_ref.flush(v.astype(BF))
C, B, F, K, R = 512, 10, 2, 2, 2
T = 2 ** B
def keys(p):
    m = (p.reshape(8, 16, C) < 0).astype(np.int64)
    return np.sum(m[:, :B] << np.arange(B)[:, None], axis=1), np.sum(m[:, B:B + F] << np.arange(F)[:, None], axis=1)
def insert(a):
    slots, free = np.full((8, T), -1), np.ones((8, C), bool)
    for k in range(K):
        for g in range(8):
            s = (a[g] + k) % T
            want = np.flatnonzero(free[g] & (slots[g][s] < 0))
            at, first = np.unique(s[want], return_index=True)
            slots[g, at] = want[first]
            free[g, want[first]] = False
    return slots
def search(slots, held, a, h):
    found = np.full((8, C), -1)
    for k in range(K):
        c = np.take_along_axis(slots, (a + k) % T, axis=1)
        hit = (found < 0) & (c >= 0) & (np.take_along_axis(held, np.maximum(c, 0), axis=1) == h)
        found[hit] = c[hit]
    return found
def numbers_of(rng):
    return {"x": np.array(f(rng, N, 128, 4 * C)), "u": np.array(f(rng, N, 128, 512)), "v": np.array(f(rng, N, 128, 512))}
def weights(rng, w):
    c, p = packed(w, rng)
    return {"wc": c, "ws": p}
def still(rng):
    w = np.zeros((N, 128, 4, 128, 4), np.float32)
    i = np.arange(128)
    for b in range(4): w[:, i, b, i, b] = 32
    return weights(rng, w.reshape(N, 128, 2048).astype(BF))
def spots(rng):
    e = np.stack([np.concatenate([[0, T - 1], 1 + rng.permutation(T - 2)[:C - 2]]) for g in range(8)])
    return rng.permuted(np.tile(e, (N, 1, 1)), axis=2)
def plant(d, rng, a, h, size, look):
    x, u = d["x"].reshape(N, 8, 16, C, 4), d["u"].reshape(N, 128, 8, 16, 4)
    k = ((a + (h << B))[..., None] >> np.arange(16)) & 1
    m = np.where(k == 1, -1.0, rng.integers(0, 2, k.shape)) * size[:, None, None, None]
    m[..., B + F:] = 0
    x[:, :, :8] = 0
    x[:, :, :4] = m.reshape(N, 8, C, 4, 4).transpose(0, 1, 3, 2, 4).astype(np.float32).astype(BF)
    u[:, :, :, :B + F] = 0
    for g in range(8):
        for i in range(B + F): u[:, 16 * g + i // 4, g, i, i % 4] = look.astype(np.float32).astype(BF)
    return {"x": x.reshape(N, 128, 4 * C), "u": u.reshape(N, 128, 512), "v": d["v"], **still(rng)}
def setup_inputs(rng):
    return {**numbers_of(rng), **weights(rng, f(rng, N, 128, 2048))}
def setup_inputs_crowd(rng):
    s = T - C // 4 - 4
    a = (s + np.repeat(np.arange(C // 2), np.tile([3, 1, 0, 4, 0, 0, 6, 2], C // 16))) % T
    a = rng.permuted(np.tile(a, (N, 8, 1)), axis=2)
    e = int(rng.integers(N))
    o = rng.permutation(8)
    m = np.where(o % 2 == 0, C // 32, rng.integers(0, C // 16, 8))
    z = (s + 3 + 8 * ((m + 1 + rng.integers(0, C // 16 - 1, 8)) % (C // 16))) % T
    a[e] = ((s + 3 + 8 * m) % T)[:, None]
    h = rng.integers(0, 2 ** F, (N, 8, C))
    b, n = (e - 1) % N, (e + 1) % N
    for g in range(8):
        if o[g] < 4:
            a[e, g, C - K:] = z[g]
            h[e, g, C - K:] = rng.permutation(2 ** F)[:K]
            j = np.flatnonzero(a[b, g] == z[g])[0]
            a[b, g, j] = a[b, g, C - 1]
            a[b, g, C - 1] = z[g]
            h[b, g, a[b, g] == z[g]] = h[e, g, C - 1]
        else:
            h[e, g, K:] = h[n, g, np.flatnonzero(a[n, g] == a[e, g, 0])[0]]
    size = np.where((np.arange(N) + rng.integers(2)) % 2 == 0, 64.0, 1.0)
    return plant(numbers_of(rng), rng, a, h, size, np.ones(N))
def setup_inputs_found(rng):
    e = int(rng.integers(N))
    a = spots(rng)
    z, c = (e + 2) % N, int(rng.integers(1, C))
    for g in range(8):
        a[z, g, np.flatnonzero(a[z, g] == 0)[0]] = a[z, g, c]
        a[z, g, c] = 0
    h = np.tile(rng.integers(0, 2 ** F, (8, 1)) * (rng.permutation(8) % 2)[:, None], (N, 1, C))
    h[e] = (h[e] + 1) % 2 ** F
    d = plant(numbers_of(rng), rng, a, h, np.ones(N), np.ones(N))
    x = d["x"].reshape(N, 128, C, 4)
    x[z, :, c] = 0
    return {**d, "x": x.reshape(N, 128, 4 * C)}
def setup_inputs_sizes(rng):
    small = (np.arange(N) + rng.integers(N)) % N < N // 2
    a = spots(rng)
    h = rng.integers(0, 2 ** F, (N, 8, C))
    return plant(numbers_of(rng), rng, a, h, np.where(small, 2.0 ** -30, 2.0 ** 27), np.where(small, 2.0 ** -30, 2.0 ** 30))
def setup_inputs_spread(rng):
    d = setup_inputs(rng)
    d["x"] = wide(rng, N, 128, 4 * C, cols=6)
    return d
def check_inputs(d):
    b = []
    for k in ("x", "u", "v"):
        a = np.abs(d[k].astype(np.float32))
        if not (np.isfinite(a).all() and ((a == 0) | (a >= 2.0 ** -30) & (a <= 2.0 ** 30)).all()): b.append("a value of " + k)
    c, s = d["wc"] & 127, np.stack([mx_ref.live(p) for p in d["ws"]])
    if (c == 127).any(): b.append("a code of wc")
    if ((s < 85) | (s > 160))[c.reshape(N, 16, 8, 512, 4).max(axis=(2, 4)) > 0].any(): b.append("a scale of ws")
    return b
def reference(x, u, v, wc, ws):
    qu = [mx_ref.quantize(u[r]) for r in range(N)]
    lay = [pk(wc[r], ws[r]) for r in range(N)]
    now = [x[r] for r in range(N)]
    for t in range(R):
        made, a, h, slots, answers = [], [], [], [], []
        for r in range(N):
            q = mx_ref.quantize(now[r])
            made.append(tile([mx_ref.matmul(pick(lay[r], np.arange(128 * b, 128 * b + 128)), q) * np.float32(0.03125) for b in range(4)]))
            mx_ref.quantize(made[r])
            i, j = keys(mx_ref.matmul(qu[r], q))
            a.append(i)
            h.append(j)
            slots.append(insert(i))
        for r in range(N):
            n = (r + 1) % N
            answers.append(mx_ref.quantize(gcols(made[n], search(slots[n], h[n], a[r], h[r]))))
        came = decode(join(*answers))
        now = [(made[r].astype(np.float32) + cut(came, r, 4 * C)).astype(BF) for r in range(N)]
    y = np.zeros((N, 128, C), np.float32)
    oc, osc = np.zeros((N, 128, 4 * C), np.uint8), np.zeros((N, 16, C), np.uint8)
    for r in range(N):
        q = mx_ref.quantize(now[r])
        y[r] = mx_ref.matmul(mx_ref.quantize(v[r]), q)
        oc[r], osc[r] = emit(q)
    return {"y": y, "oc": oc, "osc": osc}

@@ -1,0 +1,419 @@
+import numpy as np
+from concourse.bass import DstId, RemoteDMATransfer
+from concourse.mybir import dt, AluOpType as OP, ActivationFunctionType as AF
+
+F32, F16, BF, I32, U16, U8, MX = "float32", "float16", "bfloat16", "int32", "uint16", "uint8", "float8_e4m3fn_x4"
+ROUNDS = 2
+LN2 = float(np.log(2.0))
+RUN, PLACE, PRINT, EMPTY = 0, 1, 3, 16
+W_RUN, W_PLACE, W_PRINT = 32.0, 1.0, 4096.0
+BIG = 2.0 ** 18
+ORDER = [0] * 5 + [0, 1] * 2 + [1] * 5
+SCRATCH = {"psR": ("psum", [128, 2048], F32), "psS": ("psum", [128, 512], F32), "psM": ("psum", [128, 512], F32), "psA": ("psum", [128, 1024], F32)}
+for _d, _s in [
+    (BF, "xin 2048 X1 2048 X2 2048 uin 512 vin 512 P 2048 dw 2112 ones 512 me 64 m3 64 m0 128 cc 4096 ce 2048 bu 2048 bq 512 EA 1024 EB 1024 GG 512 EE 512 FG 1024"),
+    (MX, "uq 128 vq 128 wq 512 kq 1024 eq 512 xq_0 512 xq_1 512 xq_2 512 buq 512 bqq 128 eqa 256 eqb 256 pq_0 512 pq_1 512 lc_0 512 lc_1 512 gq 128 nq 128 fq 256"),
+    (U8, "us 128 vs 128 wsc 512 ks 1024 es 512 xs_0 512 xs_1 512 xs_2 512 bus 512 bqs 128 esa 256 esb 256 psc_0 512 psc_1 512 ls_0 512 ls_1 512 gsc 128 nsc 128 fs 256"),
+    (F16, "AA 512 AB 512 TA 512 TB 512"),
+    (F32, "yo 512 pF 6 iot 512 w4 128 g8 8 gg 8 gp 8 gm 8 col 11 wd 4 tw 4 w8a 8 w8w 8 w8n 8 w8s 8 w8g 8 ba 8 ba0 8 ba1 8 keep 128 kept 256 mp 256 idc 512 run 512 "
+          "from64 512 dc 8 vv 512 sy 128 sz 128 sn 256 tab_0 1088 tab_1 1088 s5 32 s6 32 r2 64 r3 64 r4 64"),
+    (I32, "pI 1 pK 6 nn 64 ii 64 r5 32 r6 32 hq_0 32 hq_1 32 qh_0 32 qh_1 32"),
+    (U16, "la_0 64 la_1 64 of1 32 of2 32 ql_0 64 ql_1 64 lo_0 32 lo_1 32 li_0 32 li_1 32"),
+]:
+    _s = _s.split()
+    for _i in range(0, len(_s), 2):
+        SCRATCH[_s[_i]] = ("sbuf", [128, int(_s[_i + 1])], _d)
+SEMAPHORES = ["sv", "sa", "sp", "sg", "ldx0", "ldx1", "ldu", "ldv", "ldw", "ldws", "ldi0", "ldi1", "sty0", "sty1", "stc0", "stc1", "sts", "sent",
+              "gotq0", "gotq1", "gotc0", "gotc1", "gotl00", "gotl01", "gotl10", "gotl11"]
+
+
+def rank_program(g, core, T, topo):
+    me = T.rank_of(core)
+    if me is None:
+        return
+    n = len(T.cores)
+    nxt, prv = T.cores[(me + 1) % n], T.cores[(me - 1) % n]
+    V, S, PE = g.vector, g.scalar, g.tensor
+    queue = {"v": V, "a": S, "p": PE, "g": g, "y": g.sync}
+    own = {"v": "sv", "a": "sa", "p": "sp", "g": "sg"}
+    count = {"sv": 0, "sa": 0, "sp": 0, "sg": 0}
+    seen = {q: {} for q in queue}
+    sent = [0]
+    late = {}
+
+    def need(q, deps):
+        for d in deps:
+            if d is not None and seen[q].get(d[0], 0) < d[1]:
+                queue[q].wait_ge(T.sem[d[0]], d[1])
+                seen[q][d[0]] = d[1]
+
+    def done(q, ins):
+        s = own[q]
+        ins.then_inc(T.sem[s], 1)
+        count[s] += 1
+        return (s, count[s])
+
+    def vec(deps, fn, *a):
+        need("v", deps)
+        return done("v", fn(*a))
+
+    def ts(deps, out, in0, s1, s2, *ops):
+        return vec(deps, V.tensor_scalar, out, in0, s1, s2, *ops)
+
+    def tt(deps, out, in0, in1, op):
+        return vec(deps, V.tensor_tensor, out, in0, in1, op)
+
+    def act(deps, out, in_, func=AF.Copy, **kw):
+        need("a", deps)
+        return done("a", S.activation(out, in_, func, **kw))
+
+    def mm(deps, out, lq, ls, rq, rs, start=True, stop=True):
+        need("p", deps)
+        return done("p", PE.matmul_mx(out, lq, ls, rq, rs, start, stop))
+
+    def iota(out, pattern, base=0, cm=0):
+        return done("g", g.iota(out, pattern, base, cm, allow_small_or_imprecise_dtypes=True))
+
+    def select(deps, out, in_, pattern, op, base=0, cm=0):
+        need("g", deps)
+        return done("g", g.affine_select(out, in_, pattern, op, 0.0, base, cm))
+
+    def dma(q, sem, out, in_, deps=()):
+        need(q, deps)
+        queue[q].dma_start(out, in_).then_inc(T.sem[sem], 16)
+        return (sem, 16)
+
+    def bits(es):
+        m = 0
+        for e in es:
+            m |= 1 << e
+        return m
+
+    def remote(deps, dst, out, in_, sem):
+        need("g", deps)
+        rid, pid = topo.addr(dst)[:2]
+        g.remote_dma(out, in_, T.sem[sem], T.sem.sent, pid, rid, topo.mask(core, dst))
+        sent[0] += len(topo.engines(core, dst))
+
+    d_x = [dma("y", "ldx0", T.xin[:, 0:1024], T.x[:, 0:1024])]
+    d_u = dma("a", "ldu", T.uin[:], T.u[:])
+    d_x.append(dma("y", "ldx1", T.xin[:, 1024:2048], T.x[:, 1024:2048]))
+    d_w = dma("y", "ldw", T.wq[:].bitcast(dt.uint8), T.wc[:])
+    d_ws = dma("y", "ldws", T.wsc[:], T.ws[:])
+    d_v = dma("y", "ldv", T.vin[:], T.v[:])
+
+    t_pI = done("g", g.iota(T.pI[:], [[0, 1]], 0, 1))
+    t_ones = vec([], V.memset, T.ones[:], 1.0)
+    t_g8 = iota(T.g8[:], [[1, 8]])
+    iota(T.gg[:], [[1, 4], [0, 2]])
+    t_gp = iota(T.gp[:], [[0, 4], [1, 2]])
+    t_m0 = select([t_ones], T.m0[:], T.ones[:, 0:128], [[0, 32], [1, 4]], OP.is_equal)
+    t_me = select([], T.me[:], T.ones[:, 0:64], [[0, 4], [1, 4], [-1, 4]], OP.is_equal)
+    t_m3 = select([], T.m3[:], T.ones[:, 0:64], [[1, 64]], OP.is_equal, -4 * PRINT)
+    t_iot = iota(T.iot[:], [[0, 16], [1, 32]], -16)
+    t_w4 = iota(T.w4[:], [[0, 32], [1, 4]])
+    t_run = iota(T.run[:], [[1, 16], [0, 32]])
+    t_z = iota(T.idc[:], [[0, 512]])
+    tabs = [iota(T.tab_0[:, 0:1024], [[0, 1024]], EMPTY)]
+    t_f64 = iota(T.from64[:], [[2, 8], [0, 64]])
+
+    def unpackers():
+        for b in range(4):
+            late["ce"] = select([], T.ce[:, 512 * b:512 * b + 512], T.ones[:], [[-1, 512]], OP.is_equal, b, 4)
+
+    t_b = vec([], V.memset, T.tw[:, 3:4], -LN2)
+    for j, (sh, am) in enumerate([(0, 15), (0, 31), (4, 7), (2, 3), (5, 3), (0, 1)]):
+        t_k = ts([t_pI], T.pK[:, j:j + 1], T.pI[:], sh, am, OP.logical_shift_right, OP.bitwise_and)
+    t_pF = vec([t_k], V.tensor_copy, T.pF[:], T.pK[:])
+    act([t_ones], T.bu[:, 0:512], T.ones[:], scale=0.0)
+    t_wb = act([t_pF, t_b], T.col[:, 0:1], T.pF[:, 0:1], AF.Exp, bias=T.tw[:, 3:4], scale=LN2)
+    for j in range(1, 4):
+        t_bu = act([], T.bu[:, 512 * j:512 * j + 512], T.ones[:], scale=0.0)
+    t_gm = ts([t_pF, t_g8], T.gm[:], T.g8[:], T.pF[:, 2:3], None, OP.is_equal)
+    t1 = ts([], T.tw[:, 0:1], T.pF[:, 0:1], 10.0, -1.0, OP.is_lt, OP.mult)
+    t2 = ts([], T.tw[:, 1:2], T.pF[:, 0:1], 10.0, None, OP.is_ge)
+    t3 = ts([], T.tw[:, 2:3], T.pF[:, 0:1], 12.0, None, OP.is_lt)
+    for j, (row, w) in enumerate([(RUN, -2048.0), (RUN, W_RUN), (PLACE, W_PLACE), (PRINT, W_PRINT)]):
+        t_wd = ts([], T.wd[:, j:j + 1], T.pF[:, 0:1], float(row), w, OP.is_equal, OP.mult)
+    t_ba = ts([t_gp], T.ba[:], T.gg[:], T.pF[:, 4:5], 2048.0, OP.is_equal, OP.mult)
+    t_r16 = ts([], T.col[:, 4:5], T.pF[:, 1:2], -16.0, None, OP.add)
+    t_end = ts([], T.col[:, 6:7], T.pF[:, 3:4], -4.0, BIG, OP.add, OP.mult)
+    t_odd = ts([], T.col[:, 9:10], T.pF[:, 5:6], -1.0, 2048.0, OP.add, OP.mult)
+    t_ba1 = tt([t_ba], T.ba1[:], T.ba[:], T.gp[:], OP.mult)
+    for look in range(2):
+        ts([t_end], T.col[:, 7 + look:8 + look], T.col[:, 6:7], 3.0 * W_PRINT + 17.0 + 1024.0 * (1 - look), None, OP.add)
+    t_end2 = ts([t_odd, t_end], T.col[:, 10:11], T.col[:, 9:10], T.col[:, 6:7], None, OP.add)
+    t_ws = ts([t_wd], T.col[:, 5:6], T.wd[:, 1:2], T.wd[:, 2:3], T.wd[:, 3:4], OP.add, OP.add)
+    t_w8g = ts([t_gm], T.w8g[:], T.gm[:], T.wd[:, 0:1], None, OP.mult)
+    t_ba0 = tt([t_ba1], T.ba0[:], T.ba[:], T.ba1[:], OP.subtract)
+    t_w8s = ts([t_ws], T.w8s[:], T.gm[:], T.col[:, 5:6], None, OP.mult)
+    t5 = ts([t_wb, t1], T.col[:, 1:2], T.col[:, 0:1], T.tw[:, 0:1], None, OP.mult)
+    t4 = ts([t3], T.col[:, 2:3], T.tw[:, 1:2], T.tw[:, 2:3], T.col[:, 0:1], OP.mult, OP.mult)
+    t_w8 = ts([t5], T.w8a[:], T.gm[:], T.col[:, 1:2], None, OP.mult)
+    t6 = ts([t4], T.col[:, 3:4], T.col[:, 2:3], -2.0 ** -13, T.col[:, 1:2], OP.mult, OP.add)
+    t_w8n = ts([t4], T.w8n[:], T.gm[:], T.col[:, 2:3], -1.0 / 512.0, OP.mult, OP.mult)
+    t_w8w = ts([t6], T.w8w[:], T.gm[:], T.col[:, 3:4], None, OP.mult)
+    for a in range(4):
+        for par in range(2):
+            c = 512 * par + 128 * a
+            t_cA = ts([t_w8, t_m0], T.cc[:, c:c + 128], T.m0[:], T.w8a[:, 2 * a + par:2 * a + par + 1], None, OP.mult)
+
+    def fill(first, src, col, deps):
+        for q in range(8):
+            t_f = act(deps, T.cc[:, first + 64 * q:first + 64 * q + 64], src[:, 0:64], scale=col[:, q:q + 1])
+        return t_f
+
+    t_cW = fill(1024, T.me, T.w8w, [t_w8w, t_me])
+    fill(1536, T.m3, T.w8n, [t_w8n, t_m3])
+    t_dig = [dma("y", "ldi%d" % j, T.idc[row:128:16, :], src[row:128:16, :], [t_z, t_run]) for j, (row, src) in enumerate(((RUN, T.run), (PLACE, T.iot)))]
+    vec([d_u], V.quantize_mx, T.uq[:], T.us[:], T.uin[:])
+    t_qx = [vec([d_x[h]], V.quantize_mx, T.xq_0[:, 256 * h:256 * h + 256], T.xs_0[:, 256 * h:256 * h + 256], T.xin[:, 1024 * h:1024 * h + 1024]) for h in range(2)]
+
+    def constants_1():
+        late["kA"] = vec([t_cA, t_cW], V.quantize_mx, T.kq[:, 0:384], T.ks[:, 0:384], T.cc[:, 0:1536])
+        late["m"] = ts([t_w4], T.keep[:], T.w4[:], T.pF[:, 3:4], 5.0 * BIG, OP.is_ge, OP.mult)
+
+    def constants_2():
+        for odd, op in enumerate((OP.is_gt, OP.is_ge)):
+            late["mp"] = ts([t_iot, t_r16], T.mp[:, 128 * odd:128 * odd + 128], T.iot[:, 0:128], T.col[:, 4:5], 4096.0, op, OP.mult)
+        m = ts([late["m"]], T.keep[:], T.keep[:], -4.0 * BIG, None, OP.add)
+        late["keep"] = ts([m, t_end2], T.keep[:, 3::4], T.w4[:, 3::4], 0.0, T.col[:, 10:11], OP.mult, OP.add)
+
+    def constants_3():
+        fill(2048, T.me, T.ba0, [t_ba0])
+        late["cR"] = fill(2560, T.me, T.ba1, [])
+        for j, base in enumerate([b + c for b in (512.3125 - BIG, 1024.0) for c in range(4)]):
+            late["dc"] = act([], T.dc[:, j:j + 1], T.pF[:, 0:1], AF.Copy, scale=4.0, bias=base)
+
+    def constants_4():
+        fill(3072, T.me, T.w8s, [t_w8s])
+        late["cS"] = fill(3584, T.me, T.w8g, [t_w8g])
+
+    def k(i):
+        return T.kq[:, 128 * i:128 * i + 128], T.ks[:, 128 * i:128 * i + 128]
+
+    def own_word(deps, out, bank, push):
+        return vec(deps, V.tensor_tensor_scan, out, bank, push, -4.0 * BIG, OP.max, OP.add)
+
+    ein = {p: len(topo.engines(p, core)) for p in (prv, nxt)}
+    free = {"psS": None, "psM": None, "psA": None, "psR": None}
+    half_bank = (T.psS, T.psM)
+    half = (slice(0, 256), slice(256, 512))
+    st = {}
+
+    def signs(t, h, dep):
+        xq, xs = T["xq_%d" % t], T["xs_%d" % t]
+        s = mm([dep, free["psS"], free["psM"]], half_bank[h][:, 0:256], T.uq[:], T.us[:], xq[:, half[h]], xs[:, half[h]])
+        st["sg", h] = act([s, t_bu], T.bu[:, 1024 * h:1024 * h + 1024:4], half_bank[h][:, 0:256], AF.Sign, bias=7.7e-34)
+        st["bq"] = act([], T.bq[:, half[h]], half_bank[h][:, 0:256], AF.Sign, bias=7.7e-34)
+
+    def bank(par, h):
+        return [(T.psA, T.psR)[h][:, 512 * par + o:512 * par + 256:2] for o in range(2)]
+
+    def addresses(h):
+        q = vec([st["sg", h]], V.quantize_mx, T.buq[:, half[h]], T.bus[:, half[h]], T.bu[:, 1024 * h:1024 * h + 1024])
+        for par in range(2):
+            st["A", par, h] = mm([q, late["kA"], free["psA"], free["psR"]], (T.psA, T.psR)[h][:, 512 * par:512 * par + 256], *k(par), T.buq[:, half[h]], T.bus[:, half[h]])
+
+    for t in range(ROUNDS):
+        B = lambda name, t=t: T["%s_%d" % (name, t)]
+        xq, xs, P, tab, la, hq = B("xq"), B("xs"), T.P, B("tab"), B("la"), B("hq")
+        r_b = [None] * 4
+
+        def layer(b, dep=None):
+            r_b[b] = mm([d_w, d_ws, free["psR"], dep], T.psR[:, 512 * b:512 * b + 512], T.wq[:, 128 * b:128 * b + 128], T.wsc[:, 128 * b:128 * b + 128], xq[:], xs[:])
+
+        def masked(par, h):
+            for o in range(2):
+                c = 256 * h + 128 * o
+                m = tt([st["A", par, h], late["mp"]], (T.AA, T.AB)[par][:, c:c + 128], bank(par, h)[o], T.mp[:, 128 * o:128 * o + 128], OP.add)
+            return m
+
+        def turned(par, h, dep):
+            return vec([dep], V.transpose, (T.TA, T.TB)[par][:, half[h]], (T.AA, T.AB)[par][:, half[h]])
+
+        def equal(par, h, dep):
+            for r in range(2):
+                for o in range(2):
+                    c = 256 * h + 128 * r
+                    e = tt([dep], (T.EA, T.EB)[par][:, 512 * r + 256 * h + o:512 * r + 256 * h + 256:2], bank(par, h)[o], (T.TA, T.TB)[par][:, c:c + 128], OP.is_equal)
+            return e
+
+        def ranks(out, deps, first, last):
+            for i, (q, s) in enumerate(((T.eqa, T.esa), (T.eqb, T.esb))):
+                for r in range(2):
+                    w = slice(128 * r, 128 * r + 128)
+                    m = mm([deps[i]], out, *k(4 + i), q[:, w], s[:, w], first and i + r == 0, last and i + r == 2)
+            return m
+
+        if t == 0:
+            signs(0, 0, t_qx[0])
+            signs(0, 1, t_qx[1])
+            constants_3()
+            constants_1()
+            addresses(0)
+            constants_2()
+        layer(2)
+        a0, a1 = masked(0, 0), masked(1, 0)
+        x0, x1 = turned(0, 0, a0), turned(1, 0, a1)
+        addresses(1)
+        e00 = equal(0, 0, x0)
+        q_bq = vec([st["bq"]], V.quantize_mx, T.bqq[:], T.bqs[:], T.bq[:])
+        e10 = equal(1, 0, x1)
+        a0, a1 = masked(0, 1), masked(1, 1)
+        if t == 0:
+            late["kR"] = vec([late["cR"]], V.quantize_mx, T.kq[:, 384:768], T.ks[:, 384:768], T.cc[:, 1536:3072])
+        layer(3)
+        mm([e00, q_bq], T.psA[:, 0:128], *k(2), T.bqq[:], T.bqs[:], True, False)
+        H = mm([late["kR"]], T.psS[:], *k(3), T.buq[:], T.bus[:])
+        x0, x1 = turned(0, 1, a0), turned(1, 1, a1)
+        e01 = equal(0, 1, x0)
+        e11 = equal(1, 1, x1)
+        q0 = vec([e01], V.quantize_mx, T.eqa[:], T.esa[:], T.EA[:])
+        q1 = vec([e11], V.quantize_mx, T.eqb[:], T.esb[:], T.EB[:])
+        Y = ranks(T.psA[:, 0:128], (q0, q1), False, True)
+        layer(0, e01)
+        layer(1, e11)
+        if t == 0:
+            constants_4()
+        t_P = [None] * 4
+        for b in (2, 3, 0, 1):
+            t_P[b] = act([r_b[b]], P[:, b:2048:4], T.psR[:, 512 * b:512 * b + 512], scale=0.03125)
+
+        def digits(c):
+            c = slice(128 * c, 128 * c + 128)
+            return tt([H, *t_dig], T.vv[:, c], T.psS[:, c], T.idc[:, c], OP.add)
+
+        vv = {3: digits(3), 2: digits(2)}
+        yw = own_word([Y, late["keep"]], T.sy[:], T.psA[:, 0:128], T.keep[:])
+        for c in range(4):
+            o1 = ts([yw, late["dc"]], T.of1[:, c:32:4], T.sy[:, 4 * c + 3::16], T.dc[:, c:c + 1], 511.6875 + BIG, OP.min, OP.add)
+        sc, q_P = None, []
+        for j in range(16):
+            b = 7 - j // 2
+            if j % 2 == 0:
+                sc = vec([tabs[t], o1, vv[b // 2], sc], V.tensor_copy, tab[:, 0:1088].indirect(T.of1[:, 4 * b:4 * b + 4]), T.vv[:, 64 * b:64 * b + 64])
+            if j < 2:
+                nn = ts([yw], T.nn[:, 32 * j:32 * j + 32], T.sy[:, 3::4], 8.0, 4093.5 + 8.0 * j + 8.0 * BIG, OP.mult, OP.add)
+            elif j == 2:
+                vv[1] = digits(1)
+            elif j == 3:
+                ii = ts([nn], T.ii[:], T.nn[:], 3, 1023, OP.logical_shift_right, OP.bitwise_and)
+            elif j == 4:
+                hx = ts([], hq[:], T.nn[:, 0:32], 7, None, OP.bitwise_and)
+            elif j == 5:
+                l1 = vec([ii], V.tensor_copy, la[:], T.ii[:])
+            elif j == 6:
+                vv[0] = free["psS"] = digits(0)
+            elif t == 0 and j == 7:
+                late["kG"] = vec([late["cS"]], V.quantize_mx, T.kq[:, 768:1024], T.ks[:, 768:1024], T.cc[:, 3072:4096])
+            elif j > 8 and j % 2:
+                i = (j - 9) // 2
+                q_P.append(vec(t_P, V.quantize_mx, B("pq")[:, 128 * i:128 * i + 128], B("psc")[:, 128 * i:128 * i + 128], P[:, 512 * i:512 * i + 512]))
+        need("g", [l1, hx])
+        rid, pid = topo.addr(nxt)[:2]
+        es = topo.engines(core, nxt)
+        m = len(es) // 2
+        g.remote_dma_fused([RemoteDMATransfer(dst_ids=[DstId(rid=rid, pnc=pid)], dma_engine_mask=bits(e), remote_sem=T.sem["gotq%d" % t], src=s, dst=d)
+                            for e, s, d in ((es[:m], la[:], B("ql")[:]), (es[m:], hq[:], B("qh")[:]))], local_sem=T.sem.sent)
+        sent[0] += len(es)
+        remote(q_P, prv, B("lc")[:].bitcast(dt.uint8), B("pq")[:].bitcast(dt.uint8), "gotc%d" % t)
+        remote(q_P, prv, B("ls")[:], B("psc")[:], "gotc%d" % t)
+        if t == 0:
+            unpackers()
+            tabs.append(iota(T.tab_1[:, 0:1024], [[0, 1024]], EMPTY))
+        em = act([sc, l1], T.EE[:], tab[:, 0:1024].indirect(la[:, 32:64]), AF.Sign, bias=0.5 - EMPTY)
+        fe = tt([sc, l1, t_f64], T.GG[:], tab[:, 0:1024].indirect(la[:, 0:32]), T.from64[:], OP.is_ge)
+        ranks(T.psA[:, 512:640], (q1, q1), True, False)
+        q_g = vec([fe], V.quantize_mx, T.gq[:], T.gsc[:], T.GG[:])
+        mm([q_g, late["kG"]], T.psA[:, 512:640], *k(7), T.gq[:], T.gsc[:], False, False)
+        q_e = vec([em], V.quantize_mx, T.nq[:], T.nsc[:], T.EE[:])
+        Z = mm([q_e], T.psA[:, 512:640], *k(7), T.nq[:], T.nsc[:], False, True)
+        n3 = free["psA"] = own_word([Z], T.sz[:], T.psA[:, 512:640], T.keep[:])
+        n4 = ts([n3], T.s6[:], T.sz[:, 3::4], -2048.0 - BIG, 2048.0, OP.not_equal, OP.mult)
+        n5 = tt([n4], T.s5[:], T.s6[:], T.ii[:, 32:64], OP.add)
+        for c in range(4):
+            o2 = ts([n5], T.of2[:, c:32:4], T.s5[:, c:32:4], T.dc[:, 4 + c:5 + c], None, OP.min)
+        got_q = ("gotq%d" % t, ein[prv])
+        ql, qh = B("ql"), B("qh")
+        sc = None
+        for j in range(16):
+            b = 7 - j // 2
+            if j % 2 == 0:
+                sc = vec([o2, em, sc], V.tensor_copy, tab[:, 0:1088].indirect(T.of2[:, 4 * b:4 * b + 4]), T.vv[:, 64 * b:64 * b + 64])
+            if t == 0 and j == 0:
+                late["dz"] = vec([], V.memset, T.dw[:, 0:2112:528], 0.0)
+            elif t == 0 and j < 3:
+                late["kept"] = vec([late["keep"]], V.tensor_copy, T.kept[:, 128 * j - 128:128 * j], T.keep[:])
+            elif t == 0 and j == 3:
+                late["vq"] = vec([d_v], V.quantize_mx, T.vq[:], T.vs[:], T.vin[:])
+            elif 6 <= j < 10:
+                i, h, look = j - 6, (j - 6) // 2, j % 2
+                f_b = ts([got_q, late["kept"]], T.kept[:, 64 * i + 3:64 * i + 64:4], qh[:, 16 * h:16 * h + 16], -2.0 * W_PRINT, T.col[:, 7 + look:8 + look], OP.mult, OP.add)
+            elif t == 0 and 10 <= j < 14:
+                i = j - 10
+                late["ke"] = vec([late["ce"]], V.quantize_mx, T.eq[:, 128 * i:128 * i + 128], T.es[:, 128 * i:128 * i + 128], T.ce[:, 512 * i:512 * i + 512])
+        win = tab[:, 0:1024]
+        f0 = vec([sc, got_q], V.tensor_copy, T.FG[:, 0:256], win.indirect(ql[:, 0:16]))
+        f1 = act([sc, got_q], T.FG[:, 256:512], win.indirect(ql[:, 32:48]))
+        act([], T.FG[:, 512:768], win.indirect(ql[:, 16:32]))
+        f2 = act([], T.FG[:, 768:1024], win.indirect(ql[:, 48:64]))
+
+        def search(h, deps):
+            w, y, c, o = (slice(m * h, m * h + m) for m in (512, 128, 32, 16))
+            q = vec(deps, V.quantize_mx, T.fq[:, y], T.fs[:, y], T.FG[:, w])
+            N = mm([q], half_bank[h][:, 0:128], *k(6), T.fq[:, y], T.fs[:, y])
+            yield
+            z = free[("psS", "psM")[h]] = own_word([N, f_b], T.sn[:, y], half_bank[h][:, 0:128], T.kept[:, y])
+            yield
+            r = T.sn[:, 128 * h + 3:128 * h + 128:4]
+            ts([z], T.r2[:, c], r, 3000.0 - BIG, None, OP.is_le)
+            z = ts([], T.r3[:, c], r, -BIG, BIG, OP.max, OP.add)
+            yield
+            z = tt([z], T.r4[:, c], T.r2[:, c], T.r3[:, c], OP.mult)
+            yield
+            z = tt([z], T.r5[:, o], T.r4[:, 32 * h:32 * h + 16], T.r4[:, 32 * h + 16:32 * h + 32], OP.max)
+            yield
+            z = ts([z], T.r6[:, o], T.r5[:, o], 1023, None, OP.bitwise_and)
+            yield
+            z = vec([z], V.tensor_copy, B("lo")[:, o], T.r6[:, o])
+            remote([z], prv, B("li")[:, o], B("lo")[:, o], "gotl%d%d" % (t, h))
+            yield
+
+        both = [search(0, [f0, f1]), search(1, [f2])]
+        for s in ORDER:
+            next(both[s])
+        got_c = ("gotc%d" % t, 2 * ein[nxt])
+        w_b = []
+        for b in range(4):
+            D = mm([t_P[b], late["ke"], got_c], T.psR[:, 512 * b:512 * b + 512], T.eq[:, 128 * b:128 * b + 128], T.es[:, 128 * b:128 * b + 128], B("lc")[:], B("ls")[:])
+            w_b.append(act([D, late["dz"]], T.dw[:, 528 * b + 1:528 * b + 513], T.psR[:, 512 * b:512 * b + 512]))
+        free["psR"] = w_b[3]
+        X = T["X%d" % (t + 1)]
+        xq, xs = T["xq_%d" % (t + 1)], T["xs_%d" % (t + 1)]
+        t_qx = []
+        for h in range(2):
+            got_l = ("gotl%d%d" % (t, h), ein[nxt])
+            for b in range(4):
+                xn = tt([got_l, w_b[b]], X[:, 1024 * h + b:1024 * h + 1024:4], T.dw[:, 528 * b:528 * b + 513].indirect(B("li")[:, 16 * h:16 * h + 16]),
+                        P[:, 1024 * h + b:1024 * h + 1024:4], OP.add)
+                if t + 1 < ROUNDS and h == 1 and b == 2:
+                    addresses(0)
+            t_qx.append(vec([xn], V.quantize_mx, xq[:, half[h]], xs[:, half[h]], X[:, 1024 * h:1024 * h + 1024]))
+            if t + 1 < ROUNDS:
+                signs(t + 1, h, t_qx[h])
+
+    ym = [mm([t_qx[h], late["vq"], free["psS"], free["psM"]], half_bank[h][:, 0:256], T.vq[:], T.vs[:], xq[:, half[h]], xs[:, half[h]]) for h in range(2)]
+    dma("y", "stc0", T.oc[:, 0:1024], xq[:, 0:256].bitcast(dt.uint8), [t_qx[0]])
+    y0 = act([ym[0]], T.yo[:, 0:256], T.psS[:, 0:256])
+    dma("a", "sty0", T.y[:, 0:256], T.yo[:, 0:256], [y0])
+    dma("y", "stc1", T.oc[:, 1024:2048], xq[:, 256:512].bitcast(dt.uint8), [t_qx[1]])
+    need("a", [t_qx[1]])
+    for j in range(4):
+        S.dma_start(T.osc[4 * j:4 * j + 4, :], xs[32 * j:32 * j + 4, :]).then_inc(T.sem.sts, 16)
+    y1 = vec([ym[1]], V.tensor_copy, T.yo[:, 256:512], T.psM[:, 0:256])
+    dma("y", "sty1", T.y[:, 256:512], T.yo[:, 256:512], [y1])
+    need("g", [(s, c) for s, c in count.items()])
+    g.wait_ge(T.sem.sent, sent[0])
+    need("y", [("stc0", 16), ("stc1", 16), ("sty1", 16)])
+    need("a", [("sty0", 16), ("sts", 64)])

@@ -2,29 +2,29 @@ import numpy as np
 from concourse.bass import DstId, RemoteDMATransfer
 from concourse.mybir import dt, AluOpType as OP, ActivationFunctionType as AF
 
-F32, F16, BF, I32, U16, U8, MX = "float32", "float16", "bfloat16", "int32", "uint16", "uint8", "float8_e4m3fn_x4"
+F32, BF, I32, U16, U8, MX = "float32", "bfloat16", "int32", "uint16", "uint8", "float8_e4m3fn_x4"
 ROUNDS = 2
 LN2 = float(np.log(2.0))
-RUN, PLACE, PRINT, EMPTY = 0, 1, 3, 16
-W_RUN, W_PLACE, W_PRINT = 32.0, 1.0, 4096.0
-BIG = 2.0 ** 18
-ORDER = [0] * 5 + [0, 1] * 2 + [1] * 5
-SCRATCH = {"psR": ("psum", [128, 2048], F32), "psS": ("psum", [128, 512], F32), "psM": ("psum", [128, 512], F32), "psA": ("psum", [128, 1024], F32)}
+HI, LO = 1, 0
+BL, BS = 2048.0, 1024.0
+ROUNDER = 1.5 * 2.0 ** 23
+SEG = [144 * s if s < 4 else 160 * (7 - s) + 16 for s in range(8)]
+SCRATCH = {k: ("psum", [128, 512], F32) for k in ("psR0", "psR1", "psS0", "psS1", "psA0", "psA1", "psL", "psH")}
 for _d, _s in [
-    (BF, "xin 2048 X1 2048 X2 2048 uin 512 vin 512 P 2048 dw 2112 ones 512 me 64 m3 64 m0 128 cc 4096 ce 2048 bu 2048 bq 512 EA 1024 EB 1024 GG 512 EE 512 FG 1024"),
-    (MX, "uq 128 vq 128 wq 512 kq 1024 eq 512 xq_0 512 xq_1 512 xq_2 512 buq 512 bqq 128 eqa 256 eqb 256 pq_0 512 pq_1 512 lc_0 512 lc_1 512 gq 128 nq 128 fq 256"),
-    (U8, "us 128 vs 128 wsc 512 ks 1024 es 512 xs_0 512 xs_1 512 xs_2 512 bus 512 bqs 128 esa 256 esb 256 psc_0 512 psc_1 512 ls_0 512 ls_1 512 gsc 128 nsc 128 fs 256"),
-    (F16, "AA 512 AB 512 TA 512 TB 512"),
-    (F32, "yo 512 pF 6 iot 512 w4 128 g8 8 gg 8 gp 8 gm 8 col 11 wd 4 tw 4 w8a 8 w8w 8 w8n 8 w8s 8 w8g 8 ba 8 ba0 8 ba1 8 keep 128 kept 256 mp 256 idc 512 run 512 "
-          "from64 512 dc 8 vv 512 sy 128 sz 128 sn 256 tab_0 1088 tab_1 1088 s5 32 s6 32 r2 64 r3 64 r4 64"),
-    (I32, "pI 1 pK 6 nn 64 ii 64 r5 32 r6 32 hq_0 32 hq_1 32 qh_0 32 qh_1 32"),
-    (U16, "la_0 64 la_1 64 of1 32 of2 32 ql_0 64 ql_1 64 lo_0 32 lo_1 32 li_0 32 li_1 32"),
+    (BF, "xin 2048 X1 2048 X2 2048 uin 512 vin 512 P 2048 dw 2112 ones 516 ce 516 cc 2048 gm 128 c16 128 t128 128 t16 768 sg 1024 A 512 Lx 32 "
+         "E 2304 cs 2304 m01 576 mk 576 FA 512 FB 512 ra 512 rb 512 pp 768"),
+    (MX, "uq 128 vq 128 wq 512 kq 512 eq 512 xq_0 512 xq_1 512 xq_2 512 sq 256 pq_0 512 pq_1 512 lc_0 512 lc_1 512"),
+    (U8, "us 128 vs 128 wsc 512 ks 512 es 512 xs_0 512 xs_1 512 xs_2 512 ss 256 psc_0 512 psc_1 512 ls_0 512 ls_1 512"),
+    (F32, "yo 512 pF 5 col 16 t8 128 k8 128 kH 128 cp0 16 cp 16 c0 16 cd 32 cA 16 cB 16 cN 16 sy 256 sh 256 win 512 vv 512 tab_0 1152 tab_1 1152 "
+          "m0 64 e0 64 o0 64 m1 64 e1 64 o1 64 m2 128 e2 128 o2 128 ps 512 FG 1024 sn 1024 rr 64"),
+    (I32, "pI 1 pK 5 n1 32 ii 32 ci 32"),
+    (U16, "ends 2 lq_0 96 lq_1 96 ql_0 96 ql_1 96 of1 32 of2 32 lo_0 32 lo_1 32 li_0 32 li_1 32"),
 ]:
     _s = _s.split()
     for _i in range(0, len(_s), 2):
         SCRATCH[_s[_i]] = ("sbuf", [128, int(_s[_i + 1])], _d)
-SEMAPHORES = ["sv", "sa", "sp", "sg", "ldx0", "ldx1", "ldu", "ldv", "ldw", "ldws", "ldi0", "ldi1", "sty0", "sty1", "stc0", "stc1", "sts", "sent",
-              "gotq0", "gotq1", "gotc0", "gotc1", "gotl00", "gotl01", "gotl10", "gotl11"]
+SEMAPHORES = ["sv", "sa", "sp", "sg", "ldx0", "ldx1", "ldu", "ldv", "ldw", "ldws", "sty0", "sty1", "stc0", "stc1", "sts", "sent", "gotq0", "gotq1",
+              "gotc00", "gotc01", "gotc10", "gotc11", "gotl00", "gotl01", "gotl10", "gotl11"]
 
 
 def rank_program(g, core, T, topo):
@@ -39,7 +39,8 @@ def rank_program(g, core, T, topo):
     count = {"sv": 0, "sa": 0, "sp": 0, "sg": 0}
     seen = {q: {} for q in queue}
     sent = [0]
-    late = {}
+    c = {}
+    st = {}
 
     def need(q, deps):
         for d in deps:
@@ -63,31 +64,36 @@ def rank_program(g, core, T, topo):
     def tt(deps, out, in0, in1, op):
         return vec(deps, V.tensor_tensor, out, in0, in1, op)
 
+    def fill(deps, out, value):
+        return vec(deps, V.memset, out, value)
+
+    def copy(deps, out, in_):
+        return vec(deps, V.tensor_copy, out, in_)
+
+    def quant(deps, q, s, in_):
+        return vec(deps, V.quantize_mx, q, s, in_)
+
+    def pick(deps, out, data, push, low):
+        return vec(deps, V.tensor_tensor_scan, out, data, push, low, OP.max, OP.add)
+
+    def chain(deps, out, factor, term):
+        return vec(deps, V.tensor_tensor_scan, out, factor, term, 0.0, OP.mult, OP.add)
+
     def act(deps, out, in_, func=AF.Copy, **kw):
         need("a", deps)
         return done("a", S.activation(out, in_, func, **kw))
 
-    def mm(deps, out, lq, ls, rq, rs, start=True, stop=True):
+    def mm(deps, out, lq, ls, rq, rs):
         need("p", deps)
-        return done("p", PE.matmul_mx(out, lq, ls, rq, rs, start, stop))
+        return done("p", PE.matmul_mx(out, lq, ls, rq, rs, True, True))
 
-    def iota(out, pattern, base=0, cm=0):
-        return done("g", g.iota(out, pattern, base, cm, allow_small_or_imprecise_dtypes=True))
-
-    def select(deps, out, in_, pattern, op, base=0, cm=0):
-        need("g", deps)
-        return done("g", g.affine_select(out, in_, pattern, op, 0.0, base, cm))
+    def iota(out, pattern, base=0):
+        return done("g", g.iota(out, pattern, base, 0, allow_small_or_imprecise_dtypes=True))
 
     def dma(q, sem, out, in_, deps=()):
         need(q, deps)
         queue[q].dma_start(out, in_).then_inc(T.sem[sem], 16)
         return (sem, 16)
-
-    def bits(es):
-        m = 0
-        for e in es:
-            m |= 1 << e
-        return m
 
     def remote(deps, dst, out, in_, sem):
         need("g", deps)
@@ -95,325 +101,369 @@ def rank_program(g, core, T, topo):
         g.remote_dma(out, in_, T.sem[sem], T.sem.sent, pid, rid, topo.mask(core, dst))
         sent[0] += len(topo.engines(core, dst))
 
-    d_x = [dma("y", "ldx0", T.xin[:, 0:1024], T.x[:, 0:1024])]
+    def cut(h, w):
+        return slice(w * h, w * h + w)
+
+    ein = {p: len(topo.engines(p, core)) for p in (prv, nxt)}
+    psR, psS, psA = (T.psR0, T.psR1), (T.psS0, T.psS1), (T.psA0, T.psA1)
+    col = lambda j: T.col[:, j:j + 1]
+    pF = lambda j: T.pF[:, j:j + 1]
+
+    d_x = {HI: dma("y", "ldx1", T.xin[:, 1024:2048], T.x[:, 1024:2048])}
     d_u = dma("a", "ldu", T.uin[:], T.u[:])
-    d_x.append(dma("y", "ldx1", T.xin[:, 1024:2048], T.x[:, 1024:2048]))
+    d_x[LO] = dma("y", "ldx0", T.xin[:, 0:1024], T.x[:, 0:1024])
     d_w = dma("y", "ldw", T.wq[:].bitcast(dt.uint8), T.wc[:])
     d_ws = dma("y", "ldws", T.wsc[:], T.ws[:])
     d_v = dma("y", "ldv", T.vin[:], T.v[:])
 
-    t_pI = done("g", g.iota(T.pI[:], [[0, 1]], 0, 1))
-    t_ones = vec([], V.memset, T.ones[:], 1.0)
-    t_g8 = iota(T.g8[:], [[1, 8]])
-    iota(T.gg[:], [[1, 4], [0, 2]])
-    t_gp = iota(T.gp[:], [[0, 4], [1, 2]])
-    t_m0 = select([t_ones], T.m0[:], T.ones[:, 0:128], [[0, 32], [1, 4]], OP.is_equal)
-    t_me = select([], T.me[:], T.ones[:, 0:64], [[0, 4], [1, 4], [-1, 4]], OP.is_equal)
-    t_m3 = select([], T.m3[:], T.ones[:, 0:64], [[1, 64]], OP.is_equal, -4 * PRINT)
-    t_iot = iota(T.iot[:], [[0, 16], [1, 32]], -16)
-    t_w4 = iota(T.w4[:], [[0, 32], [1, 4]])
-    t_run = iota(T.run[:], [[1, 16], [0, 32]])
-    t_z = iota(T.idc[:], [[0, 512]])
-    tabs = [iota(T.tab_0[:, 0:1024], [[0, 1024]], EMPTY)]
-    t_f64 = iota(T.from64[:], [[2, 8], [0, 64]])
+    c["pI"] = done("g", g.iota(T.pI[:], [[0, 1]], 0, 1))
+    c["c16"] = iota(T.c16[:], [[1, 8], [0, 16]])
+    c["cp0"] = iota(T.cp0[:], [[0, 2], [16, 8]])
+    c["t8"] = iota(T.t8[:], [[0, 16], [1, 8]])
+    c["t128"] = iota(T.t128[:], [[1, 128]])
+    c["win"] = iota(T.win[:], [[1, 512]])
+    tabs = [iota(T.tab_0[:, 0:1024], [[0, 1024]])]
+    c["t16"] = iota(T.t16[:], [[0, 48], [1, 16]])
+
+    t_b = fill([], col(0), -LN2)
+    for j, (sh, am) in enumerate([(0, 15), (4, 7), (1, 7), (0, 7), (3, 1)]):
+        z = ts([c["pI"]], T.pK[:, j:j + 1], T.pI[:], sh, am, OP.logical_shift_right, OP.bitwise_and)
+    t_eb = fill([], col(1), BL / 64.0)
+    t_pF = copy([z], T.pF[:], T.pK[:])
+    t_w = act([t_pF, t_b], col(2), pF(0), AF.Exp, bias=col(0), scale=LN2)
+    t_cz = fill([], T.cc[:], 0.0)
+    ts([t_pF], col(3), pF(0), 10.0, -1.0, OP.is_lt, OP.mult)
+    ts([], col(4), pF(0), 10.0, -2.0 ** -10, OP.is_ge, OP.mult)
+    ts([], col(5), pF(0), 12.0, None, OP.is_lt)
+    t_gm = ts([c["c16"]], T.gm[:], T.c16[:], pF(1), None, OP.is_equal)
+    c["sz"] = fill([], T.sg[:, 1::2], 0.0)
+    z = ts([c["cp0"]], T.cp[:], T.cp0[:], pF(0), None, OP.add)
+    ts([], col(6), pF(2), -2.0 * BL, BL, OP.mult, OP.add)
+    ts([], col(7), pF(2), -1.0, 7.0, OP.mult, OP.add)
+    t_o = ts([], col(8), pF(0), -1.0, 0.5, OP.mult, OP.add)
+    c["c0"] = ts([z], T.c0[:], T.cp[:], -1.0, BL + 511.5 - 1024.0, OP.mult, OP.add)
+    for k in (T.k8, T.kH):
+        t_k = ts([t_o, c["t8"]], k[:], T.t8[:], 2.0 * BL, col(6), OP.mult, OP.add)
+    z = ts([], col(9), col(7), col(7), -BL, OP.mult, OP.mult)
+    ts([t_w], col(10), col(2), col(3), None, OP.mult)
+    t_wh = ts([], col(11), col(2), col(4), col(5), OP.mult, OP.mult)
+    t_f8 = ts([z], col(9), col(9), -BL, None, OP.add)
+    for first, step, w in ((0, 4, 10), (514, 4, 10), (1024, 8, 10), (1030, 8, 10), (1536, 8, 11), (1542, 8, 11)):
+        top = first // 512 * 512 + 512
+        src = T.gm[:] if step == 4 else T.gm[:, first % 8 // 6::2]
+        t_cc = ts([t_wh, t_gm, t_cz], T.cc[:, first:top:step], src, col(w), None, OP.mult)
+    q_u = quant([d_u], T.uq[:], T.us[:], T.uin[:])
+
+    def stationaries():
+        c["k"] = quant([t_cc], T.kq[:], T.ks[:], T.cc[:])
+
+    def pushes_8():
+        ts([t_k, t_f8], T.k8[:, 7::8], T.cp[:], 0.0, col(9), OP.mult, OP.add)
+        c["k8"] = ts([], T.kH[:, 7::8], T.cp[:], 4.0, col(9), OP.mult, OP.add)
+
+    def factors_1():
+        for k in range(4):
+            ts([c["t128"]], T.m01[:, 144 * k:144 * k + 128], T.t128[:], -16.0 * k, pF(0), OP.add, OP.is_equal)
+            z = ts([], T.m01[:, 144 * k + 128:144 * k + 144], T.t128[:, 0:16], pF(0), None, OP.is_equal)
+        c["m01"] = z
+
+    def factors_2():
+        c["mk"] = ts([c["m01"]], T.mk[:], T.m01[:], 255.0, 1.0, OP.mult, OP.add)
+        ts([], col(12), pF(3), 160.0, 15.0, OP.mult, OP.add)
+        c["e"] = ts([], col(13), pF(3), -144.0, 1151.0, OP.mult, OP.add)
+        for h in range(2):
+            c["cd"] = ts([], T.cd[:, cut(h, 16)], T.cp[:], 1024.0, None, OP.add)
+
+    def factors_3():
+        fill([c["mk"]], T.mk[:, 0:576:144], 0.0)
+        c["mk"] = fill([], T.mk[:, 16:576:160], 0.0)
+        z = ts([c["e"]], col(12), col(12), col(13), None, OP.min)
+        fill([], T.m0[:, 0::2], 0.0)
+        c["e0"] = copy([c["cd"]], T.e0[:, 1::2], T.cd[:])
+        z = ts([z], col(13), pF(4), 576.0, col(12), OP.mult, OP.add)
+        fill([], T.m1[:, 0::2], 0.0)
+        c["e1"] = copy([], T.e1[:, 1::2], T.cd[:])
+        for h in range(2):
+            c["ends"] = ts([z], T.ends[:, h:h + 1], col(13), 1152.0 * h, None, OP.add)
+
+    def pushes_16():
+        c["pp"] = act([t_o, c["t16"]], T.pp[:], T.t16[:], AF.Sign, bias=col(8))
+        c["ps"] = act([c["pp"]], T.ps[:], T.pp[:, 0:512], scale=BS)
+
+    def pushes_16_last():
+        z = ts([], col(14), pF(0), -16.0, None, OP.add)
+        c["fa"] = fill([], T.FA[:, 0:128], 0.5)
+        c["fs"] = ts([z], col(15), col(14), BS, -0.125, OP.mult, OP.add)
+        c["pb"] = ts([c["pp"], c["ps"]], T.pp[:, 527::16], T.cp[:], 0.0, col(14), OP.mult, OP.add)
 
     def unpackers():
-        for b in range(4):
-            late["ce"] = select([], T.ce[:, 512 * b:512 * b + 512], T.ones[:], [[-1, 512]], OP.is_equal, b, 4)
+        z = iota(T.ones[:], [[0, 516]], 1)
+        need("g", [z])
+        c["ce"] = done("g", g.affine_select(T.ce[:], T.ones[:], [[-1, 516]], OP.is_equal, 0.0, 3, 4))
 
-    t_b = vec([], V.memset, T.tw[:, 3:4], -LN2)
-    for j, (sh, am) in enumerate([(0, 15), (0, 31), (4, 7), (2, 3), (5, 3), (0, 1)]):
-        t_k = ts([t_pI], T.pK[:, j:j + 1], T.pI[:], sh, am, OP.logical_shift_right, OP.bitwise_and)
-    t_pF = vec([t_k], V.tensor_copy, T.pF[:], T.pK[:])
-    act([t_ones], T.bu[:, 0:512], T.ones[:], scale=0.0)
-    t_wb = act([t_pF, t_b], T.col[:, 0:1], T.pF[:, 0:1], AF.Exp, bias=T.tw[:, 3:4], scale=LN2)
-    for j in range(1, 4):
-        t_bu = act([], T.bu[:, 512 * j:512 * j + 512], T.ones[:], scale=0.0)
-    t_gm = ts([t_pF, t_g8], T.gm[:], T.g8[:], T.pF[:, 2:3], None, OP.is_equal)
-    t1 = ts([], T.tw[:, 0:1], T.pF[:, 0:1], 10.0, -1.0, OP.is_lt, OP.mult)
-    t2 = ts([], T.tw[:, 1:2], T.pF[:, 0:1], 10.0, None, OP.is_ge)
-    t3 = ts([], T.tw[:, 2:3], T.pF[:, 0:1], 12.0, None, OP.is_lt)
-    for j, (row, w) in enumerate([(RUN, -2048.0), (RUN, W_RUN), (PLACE, W_PLACE), (PRINT, W_PRINT)]):
-        t_wd = ts([], T.wd[:, j:j + 1], T.pF[:, 0:1], float(row), w, OP.is_equal, OP.mult)
-    t_ba = ts([t_gp], T.ba[:], T.gg[:], T.pF[:, 4:5], 2048.0, OP.is_equal, OP.mult)
-    t_r16 = ts([], T.col[:, 4:5], T.pF[:, 1:2], -16.0, None, OP.add)
-    t_end = ts([], T.col[:, 6:7], T.pF[:, 3:4], -4.0, BIG, OP.add, OP.mult)
-    t_odd = ts([], T.col[:, 9:10], T.pF[:, 5:6], -1.0, 2048.0, OP.add, OP.mult)
-    t_ba1 = tt([t_ba], T.ba1[:], T.ba[:], T.gp[:], OP.mult)
-    for look in range(2):
-        ts([t_end], T.col[:, 7 + look:8 + look], T.col[:, 6:7], 3.0 * W_PRINT + 17.0 + 1024.0 * (1 - look), None, OP.add)
-    t_end2 = ts([t_odd, t_end], T.col[:, 10:11], T.col[:, 9:10], T.col[:, 6:7], None, OP.add)
-    t_ws = ts([t_wd], T.col[:, 5:6], T.wd[:, 1:2], T.wd[:, 2:3], T.wd[:, 3:4], OP.add, OP.add)
-    t_w8g = ts([t_gm], T.w8g[:], T.gm[:], T.wd[:, 0:1], None, OP.mult)
-    t_ba0 = tt([t_ba1], T.ba0[:], T.ba[:], T.ba1[:], OP.subtract)
-    t_w8s = ts([t_ws], T.w8s[:], T.gm[:], T.col[:, 5:6], None, OP.mult)
-    t5 = ts([t_wb, t1], T.col[:, 1:2], T.col[:, 0:1], T.tw[:, 0:1], None, OP.mult)
-    t4 = ts([t3], T.col[:, 2:3], T.tw[:, 1:2], T.tw[:, 2:3], T.col[:, 0:1], OP.mult, OP.mult)
-    t_w8 = ts([t5], T.w8a[:], T.gm[:], T.col[:, 1:2], None, OP.mult)
-    t6 = ts([t4], T.col[:, 3:4], T.col[:, 2:3], -2.0 ** -13, T.col[:, 1:2], OP.mult, OP.add)
-    t_w8n = ts([t4], T.w8n[:], T.gm[:], T.col[:, 2:3], -1.0 / 512.0, OP.mult, OP.mult)
-    t_w8w = ts([t6], T.w8w[:], T.gm[:], T.col[:, 3:4], None, OP.mult)
-    for a in range(4):
-        for par in range(2):
-            c = 512 * par + 128 * a
-            t_cA = ts([t_w8, t_m0], T.cc[:, c:c + 128], T.m0[:], T.w8a[:, 2 * a + par:2 * a + par + 1], None, OP.mult)
-
-    def fill(first, src, col, deps):
-        for q in range(8):
-            t_f = act(deps, T.cc[:, first + 64 * q:first + 64 * q + 64], src[:, 0:64], scale=col[:, q:q + 1])
-        return t_f
-
-    t_cW = fill(1024, T.me, T.w8w, [t_w8w, t_me])
-    fill(1536, T.m3, T.w8n, [t_w8n, t_m3])
-    t_dig = [dma("y", "ldi%d" % j, T.idc[row:128:16, :], src[row:128:16, :], [t_z, t_run]) for j, (row, src) in enumerate(((RUN, T.run), (PLACE, T.iot)))]
-    vec([d_u], V.quantize_mx, T.uq[:], T.us[:], T.uin[:])
-    t_qx = [vec([d_x[h]], V.quantize_mx, T.xq_0[:, 256 * h:256 * h + 256], T.xs_0[:, 256 * h:256 * h + 256], T.xin[:, 1024 * h:1024 * h + 1024]) for h in range(2)]
-
-    def constants_1():
-        late["kA"] = vec([t_cA, t_cW], V.quantize_mx, T.kq[:, 0:384], T.ks[:, 0:384], T.cc[:, 0:1536])
-        late["m"] = ts([t_w4], T.keep[:], T.w4[:], T.pF[:, 3:4], 5.0 * BIG, OP.is_ge, OP.mult)
-
-    def constants_2():
-        for odd, op in enumerate((OP.is_gt, OP.is_ge)):
-            late["mp"] = ts([t_iot, t_r16], T.mp[:, 128 * odd:128 * odd + 128], T.iot[:, 0:128], T.col[:, 4:5], 4096.0, op, OP.mult)
-        m = ts([late["m"]], T.keep[:], T.keep[:], -4.0 * BIG, None, OP.add)
-        late["keep"] = ts([m, t_end2], T.keep[:, 3::4], T.w4[:, 3::4], 0.0, T.col[:, 10:11], OP.mult, OP.add)
-
-    def constants_3():
-        fill(2048, T.me, T.ba0, [t_ba0])
-        late["cR"] = fill(2560, T.me, T.ba1, [])
-        for j, base in enumerate([b + c for b in (512.3125 - BIG, 1024.0) for c in range(4)]):
-            late["dc"] = act([], T.dc[:, j:j + 1], T.pF[:, 0:1], AF.Copy, scale=4.0, bias=base)
-
-    def constants_4():
-        fill(3072, T.me, T.w8s, [t_w8s])
-        late["cS"] = fill(3584, T.me, T.w8g, [t_w8g])
+    later = [
+        lambda: ts([], T.cA[:], T.cp[:], BS - 512.0, None, OP.add),
+        lambda: ts([], T.cB[:], T.cp[:], BS, None, OP.add),
+        lambda: ts([], T.cN[:], T.cp[:], -1.0, -BS, OP.mult, OP.add),
+        lambda: fill([], T.m2[:, 0::4], 0.0),
+        lambda: fill([], T.m2[:, 2::4], 1.0),
+        lambda: fill([], T.e2[:, 1::4], 512.0),
+        lambda: fill([], T.dw[:, 512:2112:528], 0.0),
+    ]
 
     def k(i):
-        return T.kq[:, 128 * i:128 * i + 128], T.ks[:, 128 * i:128 * i + 128]
+        return T.kq[:, cut(i, 128)], T.ks[:, cut(i, 128)]
 
-    def own_word(deps, out, bank, push):
-        return vec(deps, V.tensor_tensor_scan, out, bank, push, -4.0 * BIG, OP.max, OP.add)
+    bank = [None, None]
 
-    ein = {p: len(topo.engines(p, core)) for p in (prv, nxt)}
-    free = {"psS": None, "psM": None, "psA": None, "psR": None}
-    half_bank = (T.psS, T.psM)
-    half = (slice(0, 256), slice(256, 512))
-    st = {}
-
-    def signs(t, h, dep):
-        xq, xs = T["xq_%d" % t], T["xs_%d" % t]
-        s = mm([dep, free["psS"], free["psM"]], half_bank[h][:, 0:256], T.uq[:], T.us[:], xq[:, half[h]], xs[:, half[h]])
-        st["sg", h] = act([s, t_bu], T.bu[:, 1024 * h:1024 * h + 1024:4], half_bank[h][:, 0:256], AF.Sign, bias=7.7e-34)
-        st["bq"] = act([], T.bq[:, half[h]], half_bank[h][:, 0:256], AF.Sign, bias=7.7e-34)
-
-    def bank(par, h):
-        return [(T.psA, T.psR)[h][:, 512 * par + o:512 * par + 256:2] for o in range(2)]
-
-    def addresses(h):
-        q = vec([st["sg", h]], V.quantize_mx, T.buq[:, half[h]], T.bus[:, half[h]], T.bu[:, 1024 * h:1024 * h + 1024])
-        for par in range(2):
-            st["A", par, h] = mm([q, late["kA"], free["psA"], free["psR"]], (T.psA, T.psR)[h][:, 512 * par:512 * par + 256], *k(par), T.buq[:, half[h]], T.bus[:, half[h]])
-
-    for t in range(ROUNDS):
+    for t in range(ROUNDS + 1):
         B = lambda name, t=t: T["%s_%d" % (name, t)]
-        xq, xs, P, tab, la, hq = B("xq"), B("xs"), T.P, B("tab"), B("la"), B("hq")
-        r_b = [None] * 4
+        xq, xs, P = B("xq"), B("xs"), T.P
+        X = T.xin if t == 0 else T["X%d" % t]
+        last = t == ROUNDS
 
-        def layer(b, dep=None):
-            r_b[b] = mm([d_w, d_ws, free["psR"], dep], T.psR[:, 512 * b:512 * b + 512], T.wq[:, 128 * b:128 * b + 128], T.wsc[:, 128 * b:128 * b + 128], xq[:], xs[:])
+        def add(h, b):
+            w = slice(1024 * h + b, 1024 * h + 1024, 4)
+            st["x"] = tt([("gotl%d%d" % (t - 1, h), ein[nxt]), st["dw", LO, b]], X[:, w],
+                         T.dw[:, 528 * b:528 * b + 513].indirect(T["li_%d" % (t - 1)][:, cut(h, 16)]), P[:, w], OP.add)
 
-        def masked(par, h):
-            for o in range(2):
-                c = 256 * h + 128 * o
-                m = tt([st["A", par, h], late["mp"]], (T.AA, T.AB)[par][:, c:c + 128], bank(par, h)[o], T.mp[:, 128 * o:128 * o + 128], OP.add)
-            return m
+        def state(h):
+            st["q", h] = quant([d_x[h] if t == 0 else st["x"]], xq[:, cut(h, 256)], xs[:, cut(h, 256)], X[:, cut(h, 1024)])
 
-        def turned(par, h, dep):
-            return vec([dep], V.transpose, (T.TA, T.TB)[par][:, half[h]], (T.AA, T.AB)[par][:, half[h]])
+        if last:
+            for h in (HI, LO):
+                for b in range(4):
+                    add(h, b)
+                state(h)
+                y = mm([st["q", h], c["vq"]], psS[h][:, 0:256], T.vq[:], T.vs[:], xq[:, cut(h, 256)], xs[:, cut(h, 256)])
+                dma("y", "stc%d" % h, T.oc[:, cut(h, 1024)], xq[:, cut(h, 256)].bitcast(dt.uint8), [st["q", h]])
+                if h == HI:
+                    y = act([y], T.yo[:, cut(h, 256)], psS[h][:, 0:256])
+                    dma("a", "sty1", T.y[:, cut(h, 256)], T.yo[:, cut(h, 256)], [y])
+                else:
+                    need("a", [st["q", h]])
+                    for j in range(4):
+                        S.dma_start(T.osc[4 * j:4 * j + 4, :], xs[32 * j:32 * j + 4, :]).then_inc(T.sem.sts, 16)
+                    y = copy([y], T.yo[:, cut(h, 256)], psS[h][:, 0:256])
+                    dma("y", "sty0", T.y[:, cut(h, 256)], T.yo[:, cut(h, 256)], [y])
+            break
+        tab, lq, ql = B("tab"), B("lq"), B("ql")
 
-        def equal(par, h, dep):
-            for r in range(2):
-                for o in range(2):
-                    c = 256 * h + 128 * r
-                    e = tt([dep], (T.EA, T.EB)[par][:, 512 * r + 256 * h + o:512 * r + 256 * h + 256:2], bank(par, h)[o], (T.TA, T.TB)[par][:, c:c + 128], OP.is_equal)
-            return e
+        def scores(h):
+            st["s", h] = mm([st["q", h], q_u], psS[h][:, 0:256], T.uq[:], T.us[:], xq[:, cut(h, 256)], xs[:, cut(h, 256)])
 
-        def ranks(out, deps, first, last):
-            for i, (q, s) in enumerate(((T.eqa, T.esa), (T.eqb, T.esb))):
-                for r in range(2):
-                    w = slice(128 * r, 128 * r + 128)
-                    m = mm([deps[i]], out, *k(4 + i), q[:, w], s[:, w], first and i + r == 0, last and i + r == 2)
-            return m
+        def signs(h):
+            st["sg", h] = act([st["s", h], c["sz"]], T.sg[:, 512 * h:512 * h + 512:2], psS[h][:, 0:256], AF.Sign, bias=7.7e-34)
 
-        if t == 0:
-            signs(0, 0, t_qx[0])
-            signs(0, 1, t_qx[1])
-            constants_3()
-            constants_1()
-            addresses(0)
-            constants_2()
-        layer(2)
-        a0, a1 = masked(0, 0), masked(1, 0)
-        x0, x1 = turned(0, 0, a0), turned(1, 0, a1)
-        addresses(1)
-        e00 = equal(0, 0, x0)
-        q_bq = vec([st["bq"]], V.quantize_mx, T.bqq[:], T.bqs[:], T.bq[:])
-        e10 = equal(1, 0, x1)
-        a0, a1 = masked(0, 1), masked(1, 1)
-        if t == 0:
-            late["kR"] = vec([late["cR"]], V.quantize_mx, T.kq[:, 384:768], T.ks[:, 384:768], T.cc[:, 1536:3072])
-        layer(3)
-        mm([e00, q_bq], T.psA[:, 0:128], *k(2), T.bqq[:], T.bqs[:], True, False)
-        H = mm([late["kR"]], T.psS[:], *k(3), T.buq[:], T.bus[:])
-        x0, x1 = turned(0, 1, a0), turned(1, 1, a1)
-        e01 = equal(0, 1, x0)
-        e11 = equal(1, 1, x1)
-        q0 = vec([e01], V.quantize_mx, T.eqa[:], T.esa[:], T.EA[:])
-        q1 = vec([e11], V.quantize_mx, T.eqb[:], T.esb[:], T.EB[:])
-        Y = ranks(T.psA[:, 0:128], (q0, q1), False, True)
-        layer(0, e01)
-        layer(1, e11)
-        if t == 0:
-            constants_4()
-        t_P = [None] * 4
-        for b in (2, 3, 0, 1):
-            t_P[b] = act([r_b[b]], P[:, b:2048:4], T.psR[:, 512 * b:512 * b + 512], scale=0.03125)
+        def layer(h, b):
+            st["r", h, b] = mm([d_w, d_ws, st["q", h], bank[b % 2]], psR[b % 2][:, 0:256], T.wq[:, cut(b, 128)], T.wsc[:, cut(b, 128)], xq[:, cut(h, 256)], xs[:, cut(h, 256)])
 
-        def digits(c):
-            c = slice(128 * c, 128 * c + 128)
-            return tt([H, *t_dig], T.vv[:, c], T.psS[:, c], T.idc[:, c], OP.add)
+        def scaled(h, b):
+            st["P", h] = bank[b % 2] = act([st["r", h, b]], P[:, 1024 * h + b:1024 * h + 1024:4], psR[b % 2][:, 0:256], scale=0.03125)
 
-        vv = {3: digits(3), 2: digits(2)}
-        yw = own_word([Y, late["keep"]], T.sy[:], T.psA[:, 0:128], T.keep[:])
-        for c in range(4):
-            o1 = ts([yw, late["dc"]], T.of1[:, c:32:4], T.sy[:, 4 * c + 3::16], T.dc[:, c:c + 1], 511.6875 + BIG, OP.min, OP.add)
-        sc, q_P = None, []
-        for j in range(16):
-            b = 7 - j // 2
-            if j % 2 == 0:
-                sc = vec([tabs[t], o1, vv[b // 2], sc], V.tensor_copy, tab[:, 0:1088].indirect(T.of1[:, 4 * b:4 * b + 4]), T.vv[:, 64 * b:64 * b + 64])
-            if j < 2:
-                nn = ts([yw], T.nn[:, 32 * j:32 * j + 32], T.sy[:, 3::4], 8.0, 4093.5 + 8.0 * j + 8.0 * BIG, OP.mult, OP.add)
-            elif j == 2:
-                vv[1] = digits(1)
-            elif j == 3:
-                ii = ts([nn], T.ii[:], T.nn[:], 3, 1023, OP.logical_shift_right, OP.bitwise_and)
-            elif j == 4:
-                hx = ts([], hq[:], T.nn[:, 0:32], 7, None, OP.bitwise_and)
-            elif j == 5:
-                l1 = vec([ii], V.tensor_copy, la[:], T.ii[:])
-            elif j == 6:
-                vv[0] = free["psS"] = digits(0)
-            elif t == 0 and j == 7:
-                late["kG"] = vec([late["cS"]], V.quantize_mx, T.kq[:, 768:1024], T.ks[:, 768:1024], T.cc[:, 3072:4096])
-            elif j > 8 and j % 2:
-                i = (j - 9) // 2
-                q_P.append(vec(t_P, V.quantize_mx, B("pq")[:, 128 * i:128 * i + 128], B("psc")[:, 128 * i:128 * i + 128], P[:, 512 * i:512 * i + 512]))
-        need("g", [l1, hx])
-        rid, pid = topo.addr(nxt)[:2]
-        es = topo.engines(core, nxt)
-        m = len(es) // 2
-        g.remote_dma_fused([RemoteDMATransfer(dst_ids=[DstId(rid=rid, pnc=pid)], dma_engine_mask=bits(e), remote_sem=T.sem["gotq%d" % t], src=s, dst=d)
-                            for e, s, d in ((es[:m], la[:], B("ql")[:]), (es[m:], hq[:], B("qh")[:]))], local_sem=T.sem.sent)
-        sent[0] += len(es)
-        remote(q_P, prv, B("lc")[:].bitcast(dt.uint8), B("pq")[:].bitcast(dt.uint8), "gotc%d" % t)
-        remote(q_P, prv, B("ls")[:], B("psc")[:], "gotc%d" % t)
-        if t == 0:
-            unpackers()
-            tabs.append(iota(T.tab_1[:, 0:1024], [[0, 1024]], EMPTY))
-        em = act([sc, l1], T.EE[:], tab[:, 0:1024].indirect(la[:, 32:64]), AF.Sign, bias=0.5 - EMPTY)
-        fe = tt([sc, l1, t_f64], T.GG[:], tab[:, 0:1024].indirect(la[:, 0:32]), T.from64[:], OP.is_ge)
-        ranks(T.psA[:, 512:640], (q1, q1), True, False)
-        q_g = vec([fe], V.quantize_mx, T.gq[:], T.gsc[:], T.GG[:])
-        mm([q_g, late["kG"]], T.psA[:, 512:640], *k(7), T.gq[:], T.gsc[:], False, False)
-        q_e = vec([em], V.quantize_mx, T.nq[:], T.nsc[:], T.EE[:])
-        Z = mm([q_e], T.psA[:, 512:640], *k(7), T.nq[:], T.nsc[:], False, True)
-        n3 = free["psA"] = own_word([Z], T.sz[:], T.psA[:, 512:640], T.keep[:])
-        n4 = ts([n3], T.s6[:], T.sz[:, 3::4], -2048.0 - BIG, 2048.0, OP.not_equal, OP.mult)
-        n5 = tt([n4], T.s5[:], T.s6[:], T.ii[:, 32:64], OP.add)
-        for c in range(4):
-            o2 = ts([n5], T.of2[:, c:32:4], T.s5[:, c:32:4], T.dc[:, 4 + c:5 + c], None, OP.min)
-        got_q = ("gotq%d" % t, ein[prv])
-        ql, qh = B("ql"), B("qh")
-        sc = None
-        for j in range(16):
-            b = 7 - j // 2
-            if j % 2 == 0:
-                sc = vec([o2, em, sc], V.tensor_copy, tab[:, 0:1088].indirect(T.of2[:, 4 * b:4 * b + 4]), T.vv[:, 64 * b:64 * b + 64])
-            if t == 0 and j == 0:
-                late["dz"] = vec([], V.memset, T.dw[:, 0:2112:528], 0.0)
-            elif t == 0 and j < 3:
-                late["kept"] = vec([late["keep"]], V.tensor_copy, T.kept[:, 128 * j - 128:128 * j], T.keep[:])
-            elif t == 0 and j == 3:
-                late["vq"] = vec([d_v], V.quantize_mx, T.vq[:], T.vs[:], T.vin[:])
-            elif 6 <= j < 10:
-                i, h, look = j - 6, (j - 6) // 2, j % 2
-                f_b = ts([got_q, late["kept"]], T.kept[:, 64 * i + 3:64 * i + 64:4], qh[:, 16 * h:16 * h + 16], -2.0 * W_PRINT, T.col[:, 7 + look:8 + look], OP.mult, OP.add)
-            elif t == 0 and 10 <= j < 14:
-                i = j - 10
-                late["ke"] = vec([late["ce"]], V.quantize_mx, T.eq[:, 128 * i:128 * i + 128], T.es[:, 128 * i:128 * i + 128], T.ce[:, 512 * i:512 * i + 512])
-        win = tab[:, 0:1024]
-        f0 = vec([sc, got_q], V.tensor_copy, T.FG[:, 0:256], win.indirect(ql[:, 0:16]))
-        f1 = act([sc, got_q], T.FG[:, 256:512], win.indirect(ql[:, 32:48]))
-        act([], T.FG[:, 512:768], win.indirect(ql[:, 16:32]))
-        f2 = act([], T.FG[:, 768:1024], win.indirect(ql[:, 48:64]))
+        def keys(h):
+            q = quant([st["sg", h]], T.sq[:, cut(h, 128)], T.ss[:, cut(h, 128)], T.sg[:, cut(h, 512)])
+            for name, out, i in (("L", T.psL, 2), ("H", T.psH, 3), ("A0", T.psA0, 0), ("A1", T.psA1, 1)):
+                st[name] = mm([q, c["k"], st.get("free" + name)], out[:, 0:128], *k(i), T.sq[:, cut(h, 128)], T.ss[:, cut(h, 128)])
 
-        def search(h, deps):
-            w, y, c, o = (slice(m * h, m * h + m) for m in (512, 128, 32, 16))
-            q = vec(deps, V.quantize_mx, T.fq[:, y], T.fs[:, y], T.FG[:, w])
-            N = mm([q], half_bank[h][:, 0:128], *k(6), T.fq[:, y], T.fs[:, y])
-            yield
-            z = free[("psS", "psM")[h]] = own_word([N, f_b], T.sn[:, y], half_bank[h][:, 0:128], T.kept[:, y])
-            yield
-            r = T.sn[:, 128 * h + 3:128 * h + 128:4]
-            ts([z], T.r2[:, c], r, 3000.0 - BIG, None, OP.is_le)
-            z = ts([], T.r3[:, c], r, -BIG, BIG, OP.max, OP.add)
-            yield
-            z = tt([z], T.r4[:, c], T.r2[:, c], T.r3[:, c], OP.mult)
-            yield
-            z = tt([z], T.r5[:, o], T.r4[:, 32 * h:32 * h + 16], T.r4[:, 32 * h + 16:32 * h + 32], OP.max)
-            yield
-            z = ts([z], T.r6[:, o], T.r5[:, o], 1023, None, OP.bitwise_and)
-            yield
-            z = vec([z], V.tensor_copy, B("lo")[:, o], T.r6[:, o])
-            remote([z], prv, B("li")[:, o], B("lo")[:, o], "gotl%d%d" % (t, h))
-            yield
+        def spread(h):
+            for e in range(2):
+                st["A", h] = st["freeA%d" % e] = act([st["A%d" % e]], T.A[:, 256 * h + e:256 * h + 256:2], psA[e][:, 0:128], AF.Exp, scale=1.0 / 64.0)
 
-        both = [search(0, [f0, f1]), search(1, [f2])]
-        for s in ORDER:
-            next(both[s])
-        got_c = ("gotc%d" % t, 2 * ein[nxt])
-        w_b = []
-        for b in range(4):
-            D = mm([t_P[b], late["ke"], got_c], T.psR[:, 512 * b:512 * b + 512], T.eq[:, 128 * b:128 * b + 128], T.es[:, 128 * b:128 * b + 128], B("lc")[:], B("ls")[:])
-            w_b.append(act([D, late["dz"]], T.dw[:, 528 * b + 1:528 * b + 513], T.psR[:, 512 * b:512 * b + 512]))
-        free["psR"] = w_b[3]
-        X = T["X%d" % (t + 1)]
-        xq, xs = T["xq_%d" % (t + 1)], T["xs_%d" % (t + 1)]
-        t_qx = []
-        for h in range(2):
-            got_l = ("gotl%d%d" % (t, h), ein[nxt])
+        def lists_1(h):
+            st["sy", h] = st["freeL"] = pick([st["L"], c["k8"]], T.sy[:, cut(h, 128)], T.psL[:, 0:128], T.k8[:], -2.0 * BL)
+            st["sh", h] = st["freeH"] = pick([st["H"]], T.sh[:, cut(h, 128)], T.psH[:, 0:128], T.kH[:], -2.0 * BL)
+
+        def spread_own(h):
+            st["Lx", h] = act([st["sy", h], t_eb], T.Lx[:, cut(h, 16)], T.sy[:, 128 * h + 7:128 * h + 128:8], AF.Exp, bias=col(1), scale=1.0 / 64.0)
+
+        def lists_2(h):
+            st["lv", h] = ts([st["sh", h]], lq[:, 64 + 16 * h:80 + 16 * h], T.sh[:, 128 * h + 7:128 * h + 128:8], BL + 1.5, None, OP.add)
+            st["e0", h] = tt([c["c0"]], T.e0[:, 32 * h:32 * h + 32:2], T.sy[:, 128 * h + 7:128 * h + 128:8], T.c0[:], OP.add)
+
+        def entry(r):
+            st["vv", r] = act([st["lv", r // 2], c["win"]], T.vv[:, cut(r, 128)], T.win[:].indirect(lq[:, 64 + 8 * r:72 + 8 * r]), scale=0.25, bias=128.0 * r + 0.125)
+
+        def equal(r):
+            for s in range(8):
+                a = 576 * r + SEG[s]
+                st["E", r] = ts([st["A", r // 2], st["Lx", r // 2]], T.E[:, a:a + 16 * s + 16], T.A[:, 128 * r:128 * r + 16 * s + 16], T.Lx[:, 8 * r + s:8 * r + s + 1], None, OP.is_equal)
+
+        def earlier(r):
+            st["cs", r // 2] = chain([st["E", r], c["mk"]], T.cs[:, cut(r, 576)], T.mk[:], T.E[:, cut(r, 576)])
+
+        def first(h):
+            st["z", h] = ts([st["cs", h], c["ends"]], T.m0[:, 32 * h + 1:32 * h + 32:2], T.cs[:, cut(h, 1152)].indirect(T.ends[:, 0:1]), 128.0, None, OP.is_lt)
+
+        def slot(h, o, m, e, dep):
+            st["z", h] = chain([st["z", h], dep], o[:, cut(h, 32)], m[:, cut(h, 32)], e[:, cut(h, 32)])
+
+        def offsets(h, of, o):
+            st["of", h] = copy([st["z", h]], of[:, cut(h, 16)], o[:, 32 * h + 1:32 * h + 32:2])
+
+        def scatter(r, of, *deps):
+            st["sc"] = copy([st["of", r // 2], st["vv", r], *deps], tab[:, 0:1152].indirect(of[:, cut(r, 8)]), T.vv[:, cut(r, 128)])
+
+        def send_p(h):
+            q = quant([st["P", h]], B("pq")[:, cut(h, 256)], B("psc")[:, cut(h, 256)], P[:, cut(h, 1024)])
+            remote([q], prv, B("lc")[:, cut(h, 256)].bitcast(dt.uint8), B("pq")[:, cut(h, 256)].bitcast(dt.uint8), "gotc%d%d" % (t, h))
+            remote([q], prv, B("ls")[:, cut(h, 256)], B("psc")[:, cut(h, 256)], "gotc%d%d" % (t, h))
+
+        def unpack(h):
             for b in range(4):
-                xn = tt([got_l, w_b[b]], X[:, 1024 * h + b:1024 * h + 1024:4], T.dw[:, 528 * b:528 * b + 513].indirect(B("li")[:, 16 * h:16 * h + 16]),
-                        P[:, 1024 * h + b:1024 * h + 1024:4], OP.add)
-                if t + 1 < ROUNDS and h == 1 and b == 2:
-                    addresses(0)
-            t_qx.append(vec([xn], V.quantize_mx, xq[:, half[h]], xs[:, half[h]], X[:, 1024 * h:1024 * h + 1024]))
-            if t + 1 < ROUNDS:
-                signs(t + 1, h, t_qx[h])
+                D = mm([c["eq"], ("gotc%d%d" % (t, h), 2 * ein[nxt]), bank[b % 2]], psR[b % 2][:, 0:256], T.eq[:, cut(b, 128)], T.es[:, cut(b, 128)],
+                       B("lc")[:, cut(h, 256)], B("ls")[:, cut(h, 256)])
+                st["dw", h, b] = bank[b % 2] = act([D], T.dw[:, 528 * b + 256 * h:528 * b + 256 * h + 256], psR[b % 2][:, 0:256])
 
-    ym = [mm([t_qx[h], late["vq"], free["psS"], free["psM"]], half_bank[h][:, 0:256], T.vq[:], T.vs[:], xq[:, half[h]], xs[:, half[h]]) for h in range(2)]
-    dma("y", "stc0", T.oc[:, 0:1024], xq[:, 0:256].bitcast(dt.uint8), [t_qx[0]])
-    y0 = act([ym[0]], T.yo[:, 0:256], T.psS[:, 0:256])
-    dma("a", "sty0", T.y[:, 0:256], T.yo[:, 0:256], [y0])
-    dma("y", "stc1", T.oc[:, 1024:2048], xq[:, 256:512].bitcast(dt.uint8), [t_qx[1]])
-    need("a", [t_qx[1]])
-    for j in range(4):
-        S.dma_start(T.osc[4 * j:4 * j + 4, :], xs[32 * j:32 * j + 4, :]).then_inc(T.sem.sts, 16)
-    y1 = vec([ym[1]], V.tensor_copy, T.yo[:, 256:512], T.psM[:, 0:256])
-    dma("y", "sty1", T.y[:, 256:512], T.yo[:, 256:512], [y1])
-    need("g", [(s, c) for s, c in count.items()])
+        if t > 0:
+            for b in range(4):
+                add(HI, b)
+        state(HI)
+        scores(HI)
+        signs(HI)
+        if t == 0:
+            stationaries()
+            state(LO)
+            pushes_8()
+        for b in range(2):
+            layer(HI, b)
+            scaled(HI, b)
+            if t > 0:
+                add(LO, b)
+        keys(HI)
+        spread(HI)
+        layer(HI, 2)
+        layer(HI, 3)
+        if t > 0:
+            add(LO, 2)
+            add(LO, 3)
+        else:
+            factors_1()
+        lists_1(HI)
+        spread_own(HI)
+        if t > 0:
+            state(LO)
+        else:
+            factors_2()
+        scores(LO)
+        lists_2(HI)
+        scaled(HI, 2)
+        if t == 0:
+            factors_3()
+        entry(3)
+        signs(LO)
+        entry(2)
+        scaled(HI, 3)
+        equal(3)
+        equal(2)
+        keys(LO)
+        spread(LO)
+        earlier(3)
+        earlier(2)
+        lists_1(LO)
+        spread_own(LO)
+        first(HI)
+        lists_2(LO)
+        slot(HI, T.o0, T.m0, T.e0, c["e0"])
+        entry(1)
+        entry(0)
+        for b in range(4):
+            layer(LO, b)
+            scaled(LO, b)
+        send_p(HI)
+        offsets(HI, T.of1, T.o0)
+        equal(1)
+        scatter(3, T.of1, tabs[t])
+        equal(0)
+        scatter(2, T.of1, st["sc"])
+        earlier(1)
+        earlier(0)
+        if t == 0:
+            pushes_16()
+            unpackers()
+            tabs.append(iota(T.tab_1[:, 0:1024], [[0, 1024]]))
+        la = ts([], lq[:, 0:32], T.sy[:, 7::8], BL + 511.5, None, OP.add)
+        z1 = ts([], T.n1[:], T.sy[:, 7::8], BL + 512.5, None, OP.add)
+        first(LO)
+        z2 = ts([], T.ci[:], T.cs[:].indirect(T.ends[:]), 1.0 / 256.0, None, OP.mult)
+        z1 = ts([z1], T.ii[:], T.n1[:], 1023, None, OP.bitwise_and)
+        slot(LO, T.o0, T.m0, T.e0, None)
+        if t == 0:
+            pushes_16_last()
+        lb = copy([z1], lq[:, 32:64], T.ii[:])
+        offsets(LO, T.of1, T.o0)
+        remote([la, lb], nxt, ql[:], lq[:], "gotq%d" % t)
+        e1 = tt([c["e1"]], T.e1[:, 0::2], T.ii[:], T.cd[:], OP.subtract)
+        pa = ts([z2, c["pb"]], T.pp[:, 15:512:16], T.ci[:], -0.5, col(14), OP.mult, OP.add)
+        scatter(1, T.of1, st["sc"])
+        send_p(LO)
+        scatter(0, T.of1, st["sc"])
+        win = tab[:, 0:1024]
+        fb = {h: act([st["sc"], lb], T.FB[:, cut(h, 256)], win.indirect(lq[:, 32 + 16 * h:48 + 16 * h]), AF.Sign) for h in (HI, LO)}
+        fa = {r: ts([st["sc"], la], T.FA[:, cut(r, 128)], win.indirect(lq[:, cut(r, 8)]), 128.0 * r, 0.5, OP.is_ge, OP.mult) for r in (3, 2, 1)}
+
+        def looked(h):
+            pick([fa[2 * h + 1 if h == LO else 2 * h], pa, c["fa"]], T.ra[:, cut(h, 256)], T.FA[:, cut(h, 256)], T.pp[:, cut(h, 256)], -4.0)
+            st["z", h] = pick([fb[h]], T.rb[:, cut(h, 256)], T.FB[:, cut(h, 256)], T.pp[:, 512:768], -4.0)
+
+        def second(h):
+            w = slice(256 * h + 15, 256 * h + 256, 16)
+            st["z", h] = tt([st["z", h]], T.m1[:, 32 * h + 1:32 * h + 32:2], T.ra[:, w], T.rb[:, w], OP.is_equal)
+
+        looked(HI)
+        looked(LO)
+        second(HI)
+        second(LO)
+        slot(HI, T.o1, T.m1, T.e1, e1)
+        slot(LO, T.o1, T.m1, T.e1, None)
+        offsets(HI, T.of2, T.o1)
+        offsets(LO, T.of2, T.o1)
+        got_q = ("gotq%d" % t, ein[prv])
+        for r in (3, 2, 1, 0):
+            scatter(r, T.of2, st["sc"], fb[LO])
+            if t == 0 and r == 3:
+                for b in range(4):
+                    c["eq"] = quant([c["ce"]], T.eq[:, cut(b, 128)], T.es[:, cut(b, 128)], T.ce[:, 3 - b:515 - b])
+            if r == 3:
+                unpack(HI)
+            if t == 0 and r == 2:
+                for f in later:
+                    c["later"] = f()
+            if r == 1:
+                f_b = ts([got_q, c["fs"]], T.ps[:, 15::16], ql[:, 64:96], -0.25, col(15), OP.mult, OP.add)
+        fg = {}
+        for h in (HI, LO):
+            for look in range(2):
+                out, src = T.FG[:, cut(2 * h + look, 256)], win.indirect(ql[:, 32 * look + 16 * h:32 * look + 16 * h + 16])
+                fg[h, look] = (copy if (h, look) == (HI, 0) else act)([st["sc"], got_q], out, src)
+        unpack(LO)
+
+        def search(h):
+            for look in range(2):
+                z = pick([fg[h, look], f_b], T.sn[:, cut(2 * h + look, 256)], T.FG[:, cut(2 * h + look, 256)], T.ps[:, cut(h, 256)], -2.0 * BS)
+                yield
+            r0, r1 = (T.sn[:, 512 * h + 256 * look + 15:512 * h + 256 * look + 256:16] for look in range(2))
+            z = ts([z], T.rr[:, cut(h, 32)], T.sn[:, 512 * h + 15:512 * h + 512:16], ROUNDER, -ROUNDER, OP.add, OP.add)
+            tt([c["later"]], T.e2[:, 64 * h:64 * h + 64:4], r1, T.cA[:], OP.add)
+            tt([], T.e2[:, 64 * h + 2:64 * h + 64:4], T.cN[:], r0, OP.subtract)
+            tt([], T.e2[:, 64 * h + 3:64 * h + 64:4], r0, T.cB[:], OP.add)
+            yield
+            tt([z], T.m2[:, 64 * h + 1:64 * h + 64:4], r1, T.rr[:, 32 * h + 16:32 * h + 32], OP.is_equal)
+            z = tt([], T.m2[:, 64 * h + 3:64 * h + 64:4], r0, T.rr[:, 32 * h:32 * h + 16], OP.not_equal)
+            yield
+            z = chain([z], T.o2[:, cut(h, 64)], T.m2[:, cut(h, 64)], T.e2[:, cut(h, 64)])
+            yield
+            z = copy([z], B("lo")[:, cut(h, 16)], T.o2[:, 64 * h + 3:64 * h + 64:4])
+            remote([z], prv, B("li")[:, cut(h, 16)], B("lo")[:, cut(h, 16)], "gotl%d%d" % (t, h))
+            yield
+
+        both = {h: search(h) for h in (HI, LO)}
+        for h in [HI] * 4 + [LO, HI] * 2 + [LO] * 4:
+            next(both[h])
+        if t == 0:
+            c["vq"] = quant([d_v], T.vq[:], T.vs[:], T.vin[:])
+
+    need("g", [(s, n) for s, n in count.items()])
     g.wait_ge(T.sem.sent, sent[0])
-    need("y", [("stc0", 16), ("stc1", 16), ("sty1", 16)])
-    need("a", [("sty0", 16), ("sts", 64)])
+    need("y", [("stc0", 16), ("stc1", 16), ("sty0", 16)])
+    need("a", [("sty1", 16), ("sts", 64)])

@@ -1,5 +1,4 @@
 import numpy as np
-from concourse.bass import DstId, RemoteDMATransfer
 from concourse.mybir import dt, AluOpType as OP, ActivationFunctionType as AF
 
 F32, BF, I32, U16, U8, MX = "float32", "bfloat16", "int32", "uint16", "uint8", "float8_e4m3fn_x4"
@@ -9,22 +8,24 @@ HI, LO = 1, 0
 BL, BS = 2048.0, 1024.0
 ROUNDER = 1.5 * 2.0 ** 23
 SEG = [144 * s if s < 4 else 160 * (7 - s) + 16 for s in range(8)]
+LA, LB, LC, LS, LV = 0, 32, 64, 96, 128
+PIECES = {"v1": (LV + 16, LV + 32), "s1": (LS + 16, LV + 16), "r1": (LS + 8, LS + 16), "r0": (LA, LS + 8)}
 SCRATCH = {k: ("psum", [128, 512], F32) for k in ("psR0", "psR1", "psS0", "psS1", "psA0", "psA1", "psL", "psH")}
 for _d, _s in [
-    (BF, "xin 2048 X1 2048 X2 2048 uin 512 vin 512 P 2048 dw 2112 ones 516 ce 516 cc 2048 gm 128 c16 128 t128 128 t16 768 sg 1024 A 512 Lx 32 "
-         "E 2304 cs 2304 m01 576 mk 576 FA 512 FB 512 ra 512 rb 512 pp 768"),
+    (BF, "xin 2048 X1 2048 X2 2048 uin 512 vin 512 P 2048 dw 2112 ones 516 ce 516 cc 2048 gm 128 c16 128 t16 256 sg 1024 A 512 Lx 32 "
+         "E 2304 cs 2304 eye 32 s8 128 mk 576 FA 512 FB 512 ra 512 rb 512 pp 768"),
     (MX, "uq 128 vq 128 wq 512 kq 512 eq 512 xq_0 512 xq_1 512 xq_2 512 sq 256 pq_0 512 pq_1 512 lc_0 512 lc_1 512"),
     (U8, "us 128 vs 128 wsc 512 ks 512 es 512 xs_0 512 xs_1 512 xs_2 512 ss 256 psc_0 512 psc_1 512 ls_0 512 ls_1 512"),
-    (F32, "yo 512 pF 5 col 16 t8 128 k8 128 kH 128 cp0 16 cp 16 c0 16 cd 32 cA 16 cB 16 cN 16 sy 256 sh 256 win 512 vv 512 tab_0 1152 tab_1 1152 "
-          "m0 64 e0 64 o0 64 m1 64 e1 64 o1 64 m2 128 e2 128 o2 128 ps 512 FG 1024 sn 1024 rr 64"),
-    (I32, "pI 1 pK 5 n1 32 ii 32 ci 32"),
-    (U16, "ends 2 lq_0 96 lq_1 96 ql_0 96 ql_1 96 of1 32 of2 32 lo_0 32 lo_1 32 li_0 32 li_1 32"),
+    (F32, "yo 512 p64 1 pF 5 col 17 t8 128 k8 128 kH 128 cp0 32 cp 32 c0 16 cA 16 cB 16 cN 16 sy 256 sh 256 win 512 vv 512 tab_0 1152 tab_1 1152 "
+          "m0 64 e0 64 o0 64 m1 96 e1 96 o1 96 m2 128 e2 128 o2 128 ps 512 FG 1024 sn 1024 rr 64"),
+    (I32, "pI 1 pK 5 n1 32 ii 32"),
+    (U16, "ends 4 lq_0 160 lq_1 160 ql_0 160 ql_1 160 of2 32 li_0 32 li_1 32"),
 ]:
     _s = _s.split()
     for _i in range(0, len(_s), 2):
         SCRATCH[_s[_i]] = ("sbuf", [128, int(_s[_i + 1])], _d)
-SEMAPHORES = ["sv", "sa", "sp", "sg", "ldx0", "ldx1", "ldu", "ldv", "ldw", "ldws", "sty0", "sty1", "stc0", "stc1", "sts", "sent", "gotq0", "gotq1",
-              "gotc00", "gotc01", "gotc10", "gotc11", "gotl00", "gotl01", "gotl10", "gotl11"]
+SEMAPHORES = ["sv", "sa", "sp", "sg", "ldx0", "ldx1", "ldu", "ldv", "ldw", "ldws", "ldm", "sty0", "sty1", "sty2", "stc0", "stc1", "stc2", "sts", "sent"]
+SEMAPHORES += ["got%s%d" % (_k, _t) for _k in ("c0", "c1", *PIECES) for _t in range(ROUNDS)]
 
 
 def rank_program(g, core, T, topo):
@@ -87,24 +88,24 @@ def rank_program(g, core, T, topo):
         need("p", deps)
         return done("p", PE.matmul_mx(out, lq, ls, rq, rs, True, True))
 
-    def iota(out, pattern, base=0):
-        return done("g", g.iota(out, pattern, base, 0, allow_small_or_imprecise_dtypes=True))
+    def iota(out, pattern, base=0, cm=0):
+        return done("g", g.iota(out, pattern, base, cm, allow_small_or_imprecise_dtypes=True))
 
     def dma(q, sem, out, in_, deps=()):
         need(q, deps)
         queue[q].dma_start(out, in_).then_inc(T.sem[sem], 16)
         return (sem, 16)
 
-    def remote(deps, dst, out, in_, sem):
+    def remote(deps, out, in_, sem):
         need("g", deps)
-        rid, pid = topo.addr(dst)[:2]
-        g.remote_dma(out, in_, T.sem[sem], T.sem.sent, pid, rid, topo.mask(core, dst))
-        sent[0] += len(topo.engines(core, dst))
+        rid, pid = topo.addr(prv)[:2]
+        g.remote_dma(out, in_, T.sem[sem], T.sem.sent, pid, rid, topo.mask(core, prv))
+        sent[0] += len(topo.engines(core, prv))
 
     def cut(h, w):
         return slice(w * h, w * h + w)
 
-    ein = {p: len(topo.engines(p, core)) for p in (prv, nxt)}
+    ein = len(topo.engines(nxt, core))
     psR, psS, psA = (T.psR0, T.psR1), (T.psS0, T.psS1), (T.psA0, T.psA1)
     col = lambda j: T.col[:, j:j + 1]
     pF = lambda j: T.pF[:, j:j + 1]
@@ -116,335 +117,390 @@ def rank_program(g, core, T, topo):
     d_ws = dma("y", "ldws", T.wsc[:], T.ws[:])
     d_v = dma("y", "ldv", T.vin[:], T.v[:])
 
+    c["p64"] = iota(T.p64[:], [[0, 1]], -64, 1)
     c["pI"] = done("g", g.iota(T.pI[:], [[0, 1]], 0, 1))
     c["c16"] = iota(T.c16[:], [[1, 8], [0, 16]])
-    c["cp0"] = iota(T.cp0[:], [[0, 2], [16, 8]])
+    c["cp0"] = iota(T.cp0[:], [[0, 4], [16, 8]])
     c["t8"] = iota(T.t8[:], [[0, 16], [1, 8]])
-    c["t128"] = iota(T.t128[:], [[1, 128]])
     c["win"] = iota(T.win[:], [[1, 512]])
+    c["m0"] = iota(T.m0[:], [[0, 64]])
     tabs = [iota(T.tab_0[:, 0:1024], [[0, 1024]])]
-    c["t16"] = iota(T.t16[:], [[0, 48], [1, 16]])
+    c["ones"] = iota(T.ones[:], [[0, 516]], 1)
 
-    t_b = fill([], col(0), -LN2)
+    t_b = fill([], col(0), 63.0 * LN2)
+    t_eb = fill([], col(1), BL / 64.0)
+    fill([], T.cc[:, 0:512], 0.0)
     for j, (sh, am) in enumerate([(0, 15), (4, 7), (1, 7), (0, 7), (3, 1)]):
         z = ts([c["pI"]], T.pK[:, j:j + 1], T.pI[:], sh, am, OP.logical_shift_right, OP.bitwise_and)
-    t_eb = fill([], col(1), BL / 64.0)
+    fill([], T.cc[:, 512:1024], 0.0)
     t_pF = copy([z], T.pF[:], T.pK[:])
-    t_w = act([t_pF, t_b], col(2), pF(0), AF.Exp, bias=col(0), scale=LN2)
-    t_cz = fill([], T.cc[:], 0.0)
+    act([c["p64"]], col(2), T.p64[:], AF.Exp, scale=LN2)
+    t_w = act([t_pF, t_b], col(16), pF(1), AF.Exp, bias=col(0), scale=-16.0 * LN2)
+    t_cz = fill([], T.cc[:, 1024:2048], 0.0)
     ts([t_pF], col(3), pF(0), 10.0, -1.0, OP.is_lt, OP.mult)
-    ts([], col(4), pF(0), 10.0, -2.0 ** -10, OP.is_ge, OP.mult)
-    ts([], col(5), pF(0), 12.0, None, OP.is_lt)
+    z = ts([], col(4), pF(0), 10.0, -2.0 ** -10, OP.is_ge, OP.mult)
     t_gm = ts([c["c16"]], T.gm[:], T.c16[:], pF(1), None, OP.is_equal)
-    c["sz"] = fill([], T.sg[:, 1::2], 0.0)
-    z = ts([c["cp0"]], T.cp[:], T.cp0[:], pF(0), None, OP.add)
-    ts([], col(6), pF(2), -2.0 * BL, BL, OP.mult, OP.add)
-    ts([], col(7), pF(2), -1.0, 7.0, OP.mult, OP.add)
-    t_o = ts([], col(8), pF(0), -1.0, 0.5, OP.mult, OP.add)
-    c["c0"] = ts([z], T.c0[:], T.cp[:], -1.0, BL + 511.5 - 1024.0, OP.mult, OP.add)
-    for k in (T.k8, T.kH):
-        t_k = ts([t_o, c["t8"]], k[:], T.t8[:], 2.0 * BL, col(6), OP.mult, OP.add)
-    z = ts([], col(9), col(7), col(7), -BL, OP.mult, OP.mult)
-    ts([t_w], col(10), col(2), col(3), None, OP.mult)
-    t_wh = ts([], col(11), col(2), col(4), col(5), OP.mult, OP.mult)
-    t_f8 = ts([z], col(9), col(9), -BL, None, OP.add)
-    for first, step, w in ((0, 4, 10), (514, 4, 10), (1024, 8, 10), (1030, 8, 10), (1536, 8, 11), (1542, 8, 11)):
-        top = first // 512 * 512 + 512
-        src = T.gm[:] if step == 4 else T.gm[:, first % 8 // 6::2]
-        t_cc = ts([t_wh, t_gm, t_cz], T.cc[:, first:top:step], src, col(w), None, OP.mult)
+    t_cp = ts([c["cp0"]], T.cp[:], T.cp0[:], pF(0), None, OP.add)
+    z = ts([z], col(5), pF(0), 12.0, col(4), OP.is_lt, OP.mult)
+    ts([t_w, z], col(10), col(2), col(16), col(3), OP.mult, OP.mult)
+    t_wh = ts([], col(11), col(2), col(16), col(5), OP.mult, OP.mult)
     q_u = quant([d_u], T.uq[:], T.us[:], T.uin[:])
+    z = act([], col(6), pF(2), scale=-1.0, bias=0.5)
+    act([], col(9), pF(2), scale=BL, bias=-8.0 * BL)
+    z = act([z, c["t8"]], T.s8[:], T.t8[:], AF.Sign, bias=col(6))
+    c["c0"] = act([t_cp], T.c0[:], T.cp[:, 0:16], scale=-1.0, bias=BL + 511.5 - 1024.0)
+    for kk in (T.k8, T.kH):
+        c["k8"] = act([z], kk[:], T.s8[:], scale=BL)
+    act([c["win"]], T.sg[:, 513::2], T.win[:, 0:256], scale=0.0)
+    for at, step, w in ((0, 4, 10), (514, 4, 10), (1024, 8, 10), (1030, 8, 10), (1536, 8, 11), (1542, 8, 11)):
+        top = at // 512 * 512 + 512
+        src = T.gm[:] if step == 4 else T.gm[:, at % 8 // 6::2]
+        t_cc = ts([t_wh, t_gm, t_cz], T.cc[:, at:top:step], src, col(w), None, OP.mult)
 
-    def stationaries():
+    def constants_1():
+        act([], T.sg[:, 1:512:2], T.win[:, 0:256], scale=0.0)
+        act([], col(12), pF(3), scale=160.0, bias=15.0)
+        c["e"] = act([], col(13), pF(3), scale=-144.0, bias=1151.0)
+        c["e0"] = act([], T.e0[:, 1::2], T.cp[:], bias=1024.0)
         c["k"] = quant([t_cc], T.kq[:], T.ks[:], T.cc[:])
 
-    def pushes_8():
-        ts([t_k, t_f8], T.k8[:, 7::8], T.cp[:], 0.0, col(9), OP.mult, OP.add)
-        c["k8"] = ts([], T.kH[:, 7::8], T.cp[:], 4.0, col(9), OP.mult, OP.add)
-
     def factors_1():
-        for k in range(4):
-            ts([c["t128"]], T.m01[:, 144 * k:144 * k + 128], T.t128[:], -16.0 * k, pF(0), OP.add, OP.is_equal)
-            z = ts([], T.m01[:, 144 * k + 128:144 * k + 144], T.t128[:, 0:16], pF(0), None, OP.is_equal)
-        c["m01"] = z
+        z = ts([c["win"]], T.eye[:, 16:32], T.win[:, 0:16], pF(0), 255.0, OP.is_equal, OP.mult)
+        fill([], T.mk[:], 1.0)
+        c["mk"] = ts([z], T.eye[:, 0:16], T.eye[:, 16:32], 1.0, None, OP.add)
 
     def factors_2():
-        c["mk"] = ts([c["m01"]], T.mk[:], T.m01[:], 255.0, 1.0, OP.mult, OP.add)
-        ts([], col(12), pF(3), 160.0, 15.0, OP.mult, OP.add)
-        c["e"] = ts([], col(13), pF(3), -144.0, 1151.0, OP.mult, OP.add)
-        for h in range(2):
-            c["cd"] = ts([], T.cd[:, cut(h, 16)], T.cp[:], 1024.0, None, OP.add)
+        fill([c["mk"]], T.mk[:, 144:576:144], 0.0)
+        z = fill([], T.mk[:, 16:576:160], 0.0)
+        for s in range(8):
+            a = SEG[s] + 16 * s
+            dma("y", "ldm", T.mk[:, a:a + 16], T.eye[:, 0:16], [z])
+        ts([c["k8"]], T.k8[:, 7::8], T.cp[:, 0:16], 0.0, col(9), OP.mult, OP.add)
+        c["k8"] = ts([], T.kH[:, 7::8], T.cp[:, 0:16], 4.0, col(9), OP.mult, OP.add)
+        c["e"] = ts([c["e"]], col(12), col(12), col(13), None, OP.min)
 
-    def factors_3():
-        fill([c["mk"]], T.mk[:, 0:576:144], 0.0)
-        c["mk"] = fill([], T.mk[:, 16:576:160], 0.0)
-        z = ts([c["e"]], col(12), col(12), col(13), None, OP.min)
-        fill([], T.m0[:, 0::2], 0.0)
-        c["e0"] = copy([c["cd"]], T.e0[:, 1::2], T.cd[:])
-        z = ts([z], col(13), pF(4), 576.0, col(12), OP.mult, OP.add)
-        fill([], T.m1[:, 0::2], 0.0)
-        c["e1"] = copy([], T.e1[:, 1::2], T.cd[:])
+    def ends():
+        z = ts([c["e"]], col(13), pF(4), 576.0, col(12), OP.mult, OP.add)
+        copy([], T.ends[:, 2:3], col(12))
+        own_h(HI)
         for h in range(2):
             c["ends"] = ts([z], T.ends[:, h:h + 1], col(13), 1152.0 * h, None, OP.add)
 
-    def pushes_16():
-        c["pp"] = act([t_o, c["t16"]], T.pp[:], T.t16[:], AF.Sign, bias=col(8))
-        c["ps"] = act([c["pp"]], T.ps[:], T.pp[:, 0:512], scale=BS)
+    def pushes():
+        z = act([], col(8), pF(0), scale=-1.0, bias=0.5)
+        act([], col(14), pF(0), bias=-16.0)
+        for j in (2, 1, 0):
+            c["pp", j] = act([z, c["t16"]], T.pp[:, cut(j, 256)], T.t16[:], AF.Sign, bias=col(8))
+        for h in range(2):
+            c["ps"] = act([c["pp", 2]], T.ps[:, cut(h, 256)], T.pp[:, 512:768], scale=BS)
 
-    def pushes_16_last():
-        z = ts([], col(14), pF(0), -16.0, None, OP.add)
-        c["fa"] = fill([], T.FA[:, 0:128], 0.5)
-        c["fs"] = ts([z], col(15), col(14), BS, -0.125, OP.mult, OP.add)
-        c["pb"] = ts([c["pp"], c["ps"]], T.pp[:, 527::16], T.cp[:], 0.0, col(14), OP.mult, OP.add)
+    def terms():
+        act([], T.e1[:, 1::3], T.cp[:], scale=-1.0, bias=-1024.0)
+        c["e1"] = act([], T.e1[:, 2::3], T.cp[:], bias=1024.0)
+        act([], T.cA[:], T.cp[:, 0:16], bias=BS - 512.0)
+        act([], T.cB[:], T.cp[:, 0:16], bias=BS)
+        c["terms"] = act([], T.cN[:], T.cp[:, 0:16], scale=-1.0, bias=-BS)
+
+    def patterns():
+        iota(T.m1[:], [[0, 32], [1, 3]])
+        iota(T.m2[:], [[0, 32], [1, 2], [0, 2]])
+        c["later"] = iota(T.e2[:], [[0, 128]], 512)
 
     def unpackers():
-        z = iota(T.ones[:], [[0, 516]], 1)
-        need("g", [z])
+        need("g", [c["ones"]])
         c["ce"] = done("g", g.affine_select(T.ce[:], T.ones[:], [[-1, 516]], OP.is_equal, 0.0, 3, 4))
 
-    later = [
-        lambda: ts([], T.cA[:], T.cp[:], BS - 512.0, None, OP.add),
-        lambda: ts([], T.cB[:], T.cp[:], BS, None, OP.add),
-        lambda: ts([], T.cN[:], T.cp[:], -1.0, -BS, OP.mult, OP.add),
-        lambda: fill([], T.m2[:, 0::4], 0.0),
-        lambda: fill([], T.m2[:, 2::4], 1.0),
-        lambda: fill([], T.e2[:, 1::4], 512.0),
-        lambda: fill([], T.dw[:, 512:2112:528], 0.0),
-    ]
+    def unpacker(b):
+        c["eq", b] = quant([c["ce"]], T.eq[:, cut(b, 128)], T.es[:, cut(b, 128)], T.ce[:, 3 - b:515 - b])
 
     def k(i):
         return T.kq[:, cut(i, 128)], T.ks[:, cut(i, 128)]
 
-    bank = [None, None]
+    def own_a(h):
+        st["sy", h] = st["freeL"] = pick([st["L"], c["k8"]], T.sy[:, cut(h, 128)], T.psL[:, 0:128], T.k8[:], -2.0 * BL)
+
+    def own_h(h):
+        st["sh", h] = st["freeH"] = pick([st["H"]], T.sh[:, cut(h, 128)], T.psH[:, 0:128], T.kH[:], -2.0 * BL)
+
+    rest = []
 
     for t in range(ROUNDS + 1):
         B = lambda name, t=t: T["%s_%d" % (name, t)]
         xq, xs, P = B("xq"), B("xs"), T.P
         X = T.xin if t == 0 else T["X%d" % t]
-        last = t == ROUNDS
 
-        def add(h, b):
-            w = slice(1024 * h + b, 1024 * h + 1024, 4)
-            st["x"] = tt([("gotl%d%d" % (t - 1, h), ein[nxt]), st["dw", LO, b]], X[:, w],
-                         T.dw[:, 528 * b:528 * b + 513].indirect(T["li_%d" % (t - 1)][:, cut(h, 16)]), P[:, w], OP.add)
+        def add(b, a, e):
+            w = slice(4 * a + b, 4 * e, 4)
+            st["x"] = tt([st["li", a // 256], st["dw", b]], X[:, w], T.dw[:, 528 * b:528 * b + 513].indirect(T["li_%d" % (t - 1)][:, a // 16:e // 16]), P[:, w], OP.add)
+            if rest and b in (0, 3 if t < ROUNDS else 1):
+                rest.pop(0)()
 
-        def state(h):
-            st["q", h] = quant([d_x[h] if t == 0 else st["x"]], xq[:, cut(h, 256)], xs[:, cut(h, 256)], X[:, cut(h, 1024)])
+        def state(a, e):
+            st["q", a // 256] = quant([d_x[a // 256] if t == 0 else st["x"]], xq[:, a:e], xs[:, a:e], X[:, 4 * a:4 * e])
+            return st["q", a // 256]
 
-        if last:
-            for h in (HI, LO):
-                for b in range(4):
-                    add(h, b)
-                state(h)
-                y = mm([st["q", h], c["vq"]], psS[h][:, 0:256], T.vq[:], T.vs[:], xq[:, cut(h, 256)], xs[:, cut(h, 256)])
-                dma("y", "stc%d" % h, T.oc[:, cut(h, 1024)], xq[:, cut(h, 256)].bitcast(dt.uint8), [st["q", h]])
-                if h == HI:
-                    y = act([y], T.yo[:, cut(h, 256)], psS[h][:, 0:256])
-                    dma("a", "sty1", T.y[:, cut(h, 256)], T.yo[:, cut(h, 256)], [y])
+        if t == ROUNDS:
+            parts = ((256, 512, T.psS1), (128, 256, T.psS0), (0, 128, T.psA0))
+            add(0, 256, 512)
+            for j, (a, e, ps) in enumerate(parts):
+                for b in range(1, 4):
+                    add(b, a, e)
+                if j == 2:
+                    dma("a", "sty1", T.y[:, 128:256], T.yo[:, 128:256], [y])
                 else:
-                    need("a", [st["q", h]])
-                    for j in range(4):
-                        S.dma_start(T.osc[4 * j:4 * j + 4, :], xs[32 * j:32 * j + 4, :]).then_inc(T.sem.sts, 16)
-                    y = copy([y], T.yo[:, cut(h, 256)], psS[h][:, 0:256])
-                    dma("y", "sty0", T.y[:, cut(h, 256)], T.yo[:, cut(h, 256)], [y])
+                    z = st["x"]
+                    add(0, *parts[j + 1][:2])
+                    st["x"] = z
+                q = state(a, e)
+                y = mm([q, c["vq"]], ps[:, 0:e - a], T.vq[:], T.vs[:], xq[:, a:e], xs[:, a:e])
+                dma("y", "stc%d" % j, T.oc[:, 4 * a:4 * e], xq[:, a:e].bitcast(dt.uint8), [q])
+                if j < 2:
+                    y = act([y], T.yo[:, a:e], ps[:, 0:e - a])
+                    if j == 0:
+                        dma("a", "sty0", T.y[:, a:e], T.yo[:, a:e], [y])
+                else:
+                    need("a", [q])
+                    for i in range(4):
+                        S.dma_start(T.osc[4 * i:4 * i + 4, :], xs[32 * i:32 * i + 4, :]).then_inc(T.sem.sts, 16)
+                    y = copy([y], T.yo[:, a:e], ps[:, 0:e - a])
+                    dma("y", "sty2", T.y[:, a:e], T.yo[:, a:e], [y])
             break
         tab, lq, ql = B("tab"), B("lq"), B("ql")
+
+        def send(name, deps):
+            w = slice(*PIECES[name])
+            remote(deps, ql[:, w], lq[:, w], "got%s%d" % (name, t))
+
+        def got(name):
+            return ("got%s%d" % (name, t), ein)
 
         def scores(h):
             st["s", h] = mm([st["q", h], q_u], psS[h][:, 0:256], T.uq[:], T.us[:], xq[:, cut(h, 256)], xs[:, cut(h, 256)])
 
         def signs(h):
-            st["sg", h] = act([st["s", h], c["sz"]], T.sg[:, 512 * h:512 * h + 512:2], psS[h][:, 0:256], AF.Sign, bias=7.7e-34)
+            st["sg", h] = st["free", psS[h].name] = act([st["s", h]], T.sg[:, 512 * h:512 * h + 512:2], psS[h][:, 0:256], AF.Sign, bias=7.7e-34)
 
         def layer(h, b):
-            st["r", h, b] = mm([d_w, d_ws, st["q", h], bank[b % 2]], psR[b % 2][:, 0:256], T.wq[:, cut(b, 128)], T.wsc[:, cut(b, 128)], xq[:, cut(h, 256)], xs[:, cut(h, 256)])
-
-        def scaled(h, b):
-            st["P", h] = bank[b % 2] = act([st["r", h, b]], P[:, 1024 * h + b:1024 * h + 1024:4], psR[b % 2][:, 0:256], scale=0.03125)
+            ps = ((T.psR1, T.psS0, T.psS1, T.psR0), (T.psR0, T.psR1, T.psS1, T.psR0))[h][b]
+            r = mm([d_w, d_ws, st["q", h], st.get(("free", ps.name))], ps[:, 0:256], T.wq[:, cut(b, 128)], T.wsc[:, cut(b, 128)], xq[:, cut(h, 256)], xs[:, cut(h, 256)])
+            st["P", h] = st["free", ps.name] = act([r], P[:, 1024 * h + b:1024 * h + 1024:4], ps[:, 0:256], scale=0.03125)
 
         def keys(h):
             q = quant([st["sg", h]], T.sq[:, cut(h, 128)], T.ss[:, cut(h, 128)], T.sg[:, cut(h, 512)])
-            for name, out, i in (("L", T.psL, 2), ("H", T.psH, 3), ("A0", T.psA0, 0), ("A1", T.psA1, 1)):
+            for name, out, i in (("A0", T.psA0, 0), ("L", T.psL, 2), ("A1", T.psA1, 1), ("H", T.psH, 3)):
                 st[name] = mm([q, c["k"], st.get("free" + name)], out[:, 0:128], *k(i), T.sq[:, cut(h, 128)], T.ss[:, cut(h, 128)])
 
         def spread(h):
             for e in range(2):
                 st["A", h] = st["freeA%d" % e] = act([st["A%d" % e]], T.A[:, 256 * h + e:256 * h + 256:2], psA[e][:, 0:128], AF.Exp, scale=1.0 / 64.0)
 
-        def lists_1(h):
-            st["sy", h] = st["freeL"] = pick([st["L"], c["k8"]], T.sy[:, cut(h, 128)], T.psL[:, 0:128], T.k8[:], -2.0 * BL)
-            st["sh", h] = st["freeH"] = pick([st["H"]], T.sh[:, cut(h, 128)], T.psH[:, 0:128], T.kH[:], -2.0 * BL)
-
         def spread_own(h):
             st["Lx", h] = act([st["sy", h], t_eb], T.Lx[:, cut(h, 16)], T.sy[:, 128 * h + 7:128 * h + 128:8], AF.Exp, bias=col(1), scale=1.0 / 64.0)
 
-        def lists_2(h):
-            st["lv", h] = ts([st["sh", h]], lq[:, 64 + 16 * h:80 + 16 * h], T.sh[:, 128 * h + 7:128 * h + 128:8], BL + 1.5, None, OP.add)
-            st["e0", h] = tt([c["c0"]], T.e0[:, 32 * h:32 * h + 32:2], T.sy[:, 128 * h + 7:128 * h + 128:8], T.c0[:], OP.add)
+        def lists(h):
+            st["e0", h] = tt([c["c0"], st["sy", h]], T.e0[:, 32 * h:32 * h + 32:2], T.sy[:, 128 * h + 7:128 * h + 128:8], T.c0[:], OP.add)
+            st["lv", h] = ts([st["sh", h]], lq[:, LV + 16 * h:LV + 16 * h + 16], T.sh[:, 128 * h + 7:128 * h + 128:8], BL + 1.5, None, OP.add)
 
         def entry(r):
-            st["vv", r] = act([st["lv", r // 2], c["win"]], T.vv[:, cut(r, 128)], T.win[:].indirect(lq[:, 64 + 8 * r:72 + 8 * r]), scale=0.25, bias=128.0 * r + 0.125)
+            st["vv", r] = act([got("v1" if r > 1 else "s1"), c["win"]], T.vv[:, cut(r, 128)], T.win[:].indirect(ql[:, LV + 8 * r:LV + 8 * r + 8]), scale=0.25, bias=128.0 * r + 0.125)
 
-        def equal(r):
-            for s in range(8):
+        def equal(r, blocks=range(8)):
+            for s in blocks:
                 a = 576 * r + SEG[s]
                 st["E", r] = ts([st["A", r // 2], st["Lx", r // 2]], T.E[:, a:a + 16 * s + 16], T.A[:, 128 * r:128 * r + 16 * s + 16], T.Lx[:, 8 * r + s:8 * r + s + 1], None, OP.is_equal)
 
         def earlier(r):
-            st["cs", r // 2] = chain([st["E", r], c["mk"]], T.cs[:, cut(r, 576)], T.mk[:], T.E[:, cut(r, 576)])
+            st["cs", r] = chain([st["E", r], ("ldm", 128)], T.cs[:, cut(r, 576)], T.mk[:], T.E[:, cut(r, 576)])
 
-        def first(h):
-            st["z", h] = ts([st["cs", h], c["ends"]], T.m0[:, 32 * h + 1:32 * h + 32:2], T.cs[:, cut(h, 1152)].indirect(T.ends[:, 0:1]), 128.0, None, OP.is_lt)
+        def first(r, w, deps):
+            e = 0 if w == 2 else 2
+            return ts([st["cs", r], c["ends"], c["m0"], *deps], T.m0[:, 16 * r + 1:16 * r + 32:2], T.cs[:, 576 * r:576 * (r + w)].indirect(T.ends[:, e:e + 1]), 128.0, None, OP.is_lt)
 
-        def slot(h, o, m, e, dep):
-            st["z", h] = chain([st["z", h], dep], o[:, cut(h, 32)], m[:, cut(h, 32)], e[:, cut(h, 32)])
+        def slot(r, w, deps):
+            a = slice(16 * r, 16 * (r + w))
+            return chain(deps, T.o0[:, a], T.m0[:, a], T.e0[:, a])
 
-        def offsets(h, of, o):
-            st["of", h] = copy([st["z", h]], of[:, cut(h, 16)], o[:, 32 * h + 1:32 * h + 32:2])
+        def offsets(r, w, dep):
+            return copy([dep], lq[:, LS + 8 * r:LS + 8 * (r + w)], T.o0[:, 16 * r + 1:16 * (r + w):2])
 
         def scatter(r, of, *deps):
-            st["sc"] = copy([st["of", r // 2], st["vv", r], *deps], tab[:, 0:1152].indirect(of[:, cut(r, 8)]), T.vv[:, cut(r, 128)])
+            st["sc"] = copy([st["vv", r], *deps], tab[:, 0:1152].indirect(of), T.vv[:, cut(r, 128)])
+
+        def pack_p(r):
+            st["pq"] = quant([st["P", r // 2]], B("pq")[:, cut(r, 128)], B("psc")[:, cut(r, 128)], P[:, cut(r, 512)])
 
         def send_p(h):
-            q = quant([st["P", h]], B("pq")[:, cut(h, 256)], B("psc")[:, cut(h, 256)], P[:, cut(h, 1024)])
-            remote([q], prv, B("lc")[:, cut(h, 256)].bitcast(dt.uint8), B("pq")[:, cut(h, 256)].bitcast(dt.uint8), "gotc%d%d" % (t, h))
-            remote([q], prv, B("ls")[:, cut(h, 256)], B("psc")[:, cut(h, 256)], "gotc%d%d" % (t, h))
+            remote([st["pq"]], B("lc")[:, cut(h, 256)].bitcast(dt.uint8), B("pq")[:, cut(h, 256)].bitcast(dt.uint8), "gotc%d%d" % (h, t))
+            remote([], B("ls")[:, cut(h, 256)], B("psc")[:, cut(h, 256)], "gotc%d%d" % (h, t))
 
         def unpack(h):
-            for b in range(4):
-                D = mm([c["eq"], ("gotc%d%d" % (t, h), 2 * ein[nxt]), bank[b % 2]], psR[b % 2][:, 0:256], T.eq[:, cut(b, 128)], T.es[:, cut(b, 128)],
+            for b, ps in enumerate(psR + psA):
+                D = mm([c["eq", b], ("gotc%d%d" % (h, t), 2 * ein), st["pq"], st.get(("dw", b))], ps[:, 0:256], T.eq[:, cut(b, 128)], T.es[:, cut(b, 128)],
                        B("lc")[:, cut(h, 256)], B("ls")[:, cut(h, 256)])
-                st["dw", h, b] = bank[b % 2] = act([D], T.dw[:, 528 * b + 256 * h:528 * b + 256 * h + 256], psR[b % 2][:, 0:256])
+                st["dw", b] = act([D], T.dw[:, 528 * b + 256 * h:528 * b + 256 * h + 256], ps[:, 0:256])
+            st["freeA0"] = st["freeA1"] = st["dw", 3]
 
         if t > 0:
             for b in range(4):
-                add(HI, b)
-        state(HI)
+                add(b, 256, 512)
+        state(256, 512)
         scores(HI)
         signs(HI)
         if t == 0:
-            stationaries()
-            state(LO)
-            pushes_8()
-        for b in range(2):
-            layer(HI, b)
-            scaled(HI, b)
-            if t > 0:
-                add(LO, b)
+            constants_1()
+            state(0, 256)
+            factors_1()
+        else:
+            layer(HI, 0)
+            layer(HI, 1)
+            for b in range(3):
+                add(b, 0, 256)
         keys(HI)
         spread(HI)
-        layer(HI, 2)
-        layer(HI, 3)
         if t > 0:
-            add(LO, 2)
-            add(LO, 3)
-        else:
-            factors_1()
-        lists_1(HI)
-        spread_own(HI)
-        if t > 0:
-            state(LO)
+            add(3, 0, 256)
+            own_a(HI)
+            state(0, 256)
+            own_h(HI)
         else:
             factors_2()
+            own_a(HI)
+            ends()
         scores(LO)
-        lists_2(HI)
-        scaled(HI, 2)
-        if t == 0:
-            factors_3()
-        entry(3)
+        spread_own(HI)
         signs(LO)
-        entry(2)
-        scaled(HI, 3)
+        for b in range(3) if t == 0 else (2, 3):
+            layer(HI, b)
+        lists(HI)
+        send("v1", [st["lv", HI]])
+        if t == 0:
+            c["t16"] = iota(T.t16[:], [[0, 16], [1, 16]])
         equal(3)
-        equal(2)
+        equal(2, range(2))
         keys(LO)
         spread(LO)
+        equal(2, range(2, 8))
         earlier(3)
-        earlier(2)
-        lists_1(LO)
+        own_a(LO)
         spread_own(LO)
-        first(HI)
-        lists_2(LO)
-        slot(HI, T.o0, T.m0, T.e0, c["e0"])
-        entry(1)
-        entry(0)
+        if t == 0:
+            layer(HI, 3)
+        earlier(2)
+        own_h(LO)
+        z = first(2, 2, [])
+        lists(LO)
+        equal(1, range(1))
+        z = slot(2, 2, [z, c["e0"]])
         for b in range(4):
             layer(LO, b)
-            scaled(LO, b)
-        send_p(HI)
-        offsets(HI, T.of1, T.o0)
-        equal(1)
-        scatter(3, T.of1, tabs[t])
-        equal(0)
-        scatter(2, T.of1, st["sc"])
-        earlier(1)
-        earlier(0)
+        entry(3)
+        entry(2)
+        equal(1, range(1, 4))
+        z = offsets(2, 2, z)
+        send("s1", [z])
         if t == 0:
-            pushes_16()
             unpackers()
-            tabs.append(iota(T.tab_1[:, 0:1024], [[0, 1024]]))
-        la = ts([], lq[:, 0:32], T.sy[:, 7::8], BL + 511.5, None, OP.add)
-        z1 = ts([], T.n1[:], T.sy[:, 7::8], BL + 512.5, None, OP.add)
-        first(LO)
-        z2 = ts([], T.ci[:], T.cs[:].indirect(T.ends[:]), 1.0 / 256.0, None, OP.mult)
-        z1 = ts([z1], T.ii[:], T.n1[:], 1023, None, OP.bitwise_and)
-        slot(LO, T.o0, T.m0, T.e0, None)
+        equal(1, range(4, 8))
+        equal(0, range(3))
+        earlier(1)
+        equal(0, range(3, 6))
+        z = first(1, 1, [])
+        equal(0, range(6, 8))
+        z2 = ts([], T.n1[:], T.sy[:, 7::8], BL + 512.5, None, OP.add)
+        z = z1 = slot(1, 1, [z])
+        ts([], lq[:, LA:LA + 32], T.sy[:, 7::8], BL + 511.5, None, OP.add)
+        earlier(0)
+        z = offsets(1, 1, z)
+        send("r1", [z])
+        entry(1)
+        entry(0)
+        z2 = ts([z2], T.ii[:], T.n1[:], 1023, None, OP.bitwise_and)
         if t == 0:
-            pushes_16_last()
-        lb = copy([z1], lq[:, 32:64], T.ii[:])
-        offsets(LO, T.of1, T.o0)
-        remote([la, lb], nxt, ql[:], lq[:], "gotq%d" % t)
-        e1 = tt([c["e1"]], T.e1[:, 0::2], T.ii[:], T.cd[:], OP.subtract)
-        pa = ts([z2, c["pb"]], T.pp[:, 15:512:16], T.ci[:], -0.5, col(14), OP.mult, OP.add)
-        scatter(1, T.of1, st["sc"])
+            pushes()
+            fill([], T.FA[:, 0:128], 0.5)
+        z = first(0, 1, [z1])
+        ts([], lq[:, LC:LC + 32], T.cs[:].indirect(T.ends[:, 0:2]), 1.0 / 256.0, None, OP.mult)
+        copy([z2], lq[:, LB:LB + 32], T.ii[:])
+        z = slot(0, 1, [z])
+        pack_p(3)
+        z = offsets(0, 1, z)
+        send("r0", [z])
+        scatter(3, ql[:, LS + 24:LS + 32], tabs[t], got("s1"))
+        pack_p(2)
+        send_p(HI)
+        if t == 0:
+            patterns()
+        scatter(2, ql[:, LS + 16:LS + 24], st["sc"])
+        pack_p(1)
+        if t == 0:
+            unpacker(0)
+            unpacker(1)
+        scatter(1, ql[:, LS + 8:LS + 16], st["sc"], got("r1"))
+        pack_p(0)
         send_p(LO)
-        scatter(0, T.of1, st["sc"])
+        if t == 0:
+            tabs.append(iota(T.tab_1[:, 0:1024], [[0, 1024]]))
+        scatter(0, ql[:, LS:LS + 8], st["sc"], got("r0"))
+        pa = ts([c["pp", 0]], T.pp[:, 15:512:16], ql[:, LC:LC + 32], -0.5, col(14), OP.mult, OP.add)
+        e1 = copy([c["later"]], T.e1[:, 0::3], ql[:, LB:LB + 32])
+        if t == 0:
+            ts([], col(15), col(14), BS, -0.125, OP.mult, OP.add)
         win = tab[:, 0:1024]
-        fb = {h: act([st["sc"], lb], T.FB[:, cut(h, 256)], win.indirect(lq[:, 32 + 16 * h:48 + 16 * h]), AF.Sign) for h in (HI, LO)}
-        fa = {r: ts([st["sc"], la], T.FA[:, cut(r, 128)], win.indirect(lq[:, cut(r, 8)]), 128.0 * r, 0.5, OP.is_ge, OP.mult) for r in (3, 2, 1)}
+        fb = {h: act([st["sc"]], T.FB[:, cut(h, 256)], win.indirect(ql[:, LB + 16 * h:LB + 16 * h + 16]), AF.Sign) for h in (HI, LO)}
+        if t == 0:
+            terms()
 
-        def looked(h):
-            pick([fa[2 * h + 1 if h == LO else 2 * h], pa, c["fa"]], T.ra[:, cut(h, 256)], T.FA[:, cut(h, 256)], T.pp[:, cut(h, 256)], -4.0)
-            st["z", h] = pick([fb[h]], T.rb[:, cut(h, 256)], T.FB[:, cut(h, 256)], T.pp[:, 512:768], -4.0)
+        def inside(r):
+            return ts([st["sc"]], T.FA[:, cut(r, 128)], win.indirect(ql[:, LA + 8 * r:LA + 8 * r + 8]), 128.0 * r, 0.5, OP.is_ge, OP.mult)
 
-        def second(h):
+        def second(h, z):
+            pick([z, pa], T.ra[:, cut(h, 256)], T.FA[:, cut(h, 256)], T.pp[:, cut(h, 256)], -4.0)
+            yield
+            z = pick([fb[h], c["pb"]], T.rb[:, cut(h, 256)], T.FB[:, cut(h, 256)], T.pp[:, 512:768], -4.0)
+            yield
             w = slice(256 * h + 15, 256 * h + 256, 16)
-            st["z", h] = tt([st["z", h]], T.m1[:, 32 * h + 1:32 * h + 32:2], T.ra[:, w], T.rb[:, w], OP.is_equal)
+            z = tt([z], T.m1[:, 48 * h + 2:48 * h + 48:3], T.ra[:, w], T.rb[:, w], OP.is_equal)
+            yield
+            z = chain([z, e1, c["e1"]], T.o1[:, cut(h, 48)], T.m1[:, cut(h, 48)], T.e1[:, cut(h, 48)])
+            yield
+            st["of", h] = copy([z], T.of2[:, cut(h, 16)], T.o1[:, 48 * h + 2:48 * h + 48:3])
+            yield
 
-        looked(HI)
-        looked(LO)
-        second(HI)
-        second(LO)
-        slot(HI, T.o1, T.m1, T.e1, e1)
-        slot(LO, T.o1, T.m1, T.e1, None)
-        offsets(HI, T.of2, T.o1)
-        offsets(LO, T.of2, T.o1)
-        got_q = ("gotq%d" % t, ein[prv])
+        inside(3)
+        z = inside(2)
+        if t == 0:
+            c["pb"] = ts([c["ps"]], T.pp[:, 527::16], T.cp[:, 0:16], 0.0, col(14), OP.mult, OP.add)
+        both = {HI: second(HI, z), LO: second(LO, inside(1))}
+        for h in (HI, HI, LO, HI, LO, HI, LO, HI, LO):
+            next(both[h])
         for r in (3, 2, 1, 0):
-            scatter(r, T.of2, st["sc"], fb[LO])
-            if t == 0 and r == 3:
-                for b in range(4):
-                    c["eq"] = quant([c["ce"]], T.eq[:, cut(b, 128)], T.es[:, cut(b, 128)], T.ce[:, 3 - b:515 - b])
+            scatter(r, T.of2[:, cut(r, 8)], st["sc"], fb[LO], st["of", r // 2])
             if r == 3:
+                next(both[LO])
+                if t == 0:
+                    unpacker(2)
+                    unpacker(3)
                 unpack(HI)
+            if r == 2:
+                f_b = ts([], T.ps[:, 15::16], lq[:, LV:LV + 32], -0.25, col(15), OP.mult, OP.add)
             if t == 0 and r == 2:
-                for f in later:
-                    c["later"] = f()
-            if r == 1:
-                f_b = ts([got_q, c["fs"]], T.ps[:, 15::16], ql[:, 64:96], -0.25, col(15), OP.mult, OP.add)
+                fill([], T.dw[:, 512:2112:528], 0.0)
+            if t == 0 and r == 1:
+                c["vq"] = quant([d_v], T.vq[:], T.vs[:], T.vin[:])
         fg = {}
         for h in (HI, LO):
             for look in range(2):
-                out, src = T.FG[:, cut(2 * h + look, 256)], win.indirect(ql[:, 32 * look + 16 * h:32 * look + 16 * h + 16])
-                fg[h, look] = (copy if (h, look) == (HI, 0) else act)([st["sc"], got_q], out, src)
+                a = LA + 32 * look + 16 * h
+                fg[h, look] = (copy if (h, look) == (HI, 0) else act)([st["sc"]], T.FG[:, cut(2 * h + look, 256)], win.indirect(lq[:, a:a + 16]))
         unpack(LO)
 
-        def search(h):
+        def search(h, B=B, fg=fg, f_b=f_b):
             for look in range(2):
                 z = pick([fg[h, look], f_b], T.sn[:, cut(2 * h + look, 256)], T.FG[:, cut(2 * h + look, 256)], T.ps[:, cut(h, 256)], -2.0 * BS)
                 yield
             r0, r1 = (T.sn[:, 512 * h + 256 * look + 15:512 * h + 256 * look + 256:16] for look in range(2))
             z = ts([z], T.rr[:, cut(h, 32)], T.sn[:, 512 * h + 15:512 * h + 512:16], ROUNDER, -ROUNDER, OP.add, OP.add)
-            tt([c["later"]], T.e2[:, 64 * h:64 * h + 64:4], r1, T.cA[:], OP.add)
+            tt([c["terms"]], T.e2[:, 64 * h:64 * h + 64:4], r1, T.cA[:], OP.add)
             tt([], T.e2[:, 64 * h + 2:64 * h + 64:4], T.cN[:], r0, OP.subtract)
             tt([], T.e2[:, 64 * h + 3:64 * h + 64:4], r0, T.cB[:], OP.add)
             yield
@@ -453,17 +509,15 @@ def rank_program(g, core, T, topo):
             yield
             z = chain([z], T.o2[:, cut(h, 64)], T.m2[:, cut(h, 64)], T.e2[:, cut(h, 64)])
             yield
-            z = copy([z], B("lo")[:, cut(h, 16)], T.o2[:, 64 * h + 3:64 * h + 64:4])
-            remote([z], prv, B("li")[:, cut(h, 16)], B("lo")[:, cut(h, 16)], "gotl%d%d" % (t, h))
+            st["li", h] = copy([z], B("li")[:, cut(h, 16)], T.o2[:, 64 * h + 3:64 * h + 64:4])
             yield
 
         both = {h: search(h) for h in (HI, LO)}
-        for h in [HI] * 4 + [LO, HI] * 2 + [LO] * 4:
+        for h in (HI, HI, LO, HI, HI, LO, HI, LO, HI, LO):
             next(both[h])
-        if t == 0:
-            c["vq"] = quant([d_v], T.vq[:], T.vs[:], T.vin[:])
+        rest += [lambda s=both[LO]: next(s)] * 2
 
     need("g", [(s, n) for s, n in count.items()])
     g.wait_ge(T.sem.sent, sent[0])
-    need("y", [("stc0", 16), ("stc1", 16), ("sty0", 16)])
-    need("a", [("sty1", 16), ("sts", 64)])
+    need("y", [("stc0", 16), ("stc1", 16), ("stc2", 16), ("sty2", 16)])
+    need("a", [("sty0", 16), ("sty1", 16), ("sts", 64)])

import numpy as np
from concourse.mybir import dt, AluOpType as OP, ActivationFunctionType as AF

F32, BF, I32, U16, U8, MX = "float32", "bfloat16", "int32", "uint16", "uint8", "float8_e4m3fn_x4"
ROUNDS = 2
LN2 = float(np.log(2.0))
HI, LO = 1, 0
BL, BS = 2048.0, 1024.0
ROUNDER = 1.5 * 2.0 ** 23
SEG = [144 * s if s < 4 else 160 * (7 - s) + 16 for s in range(8)]
LA, LB, LC, LS, LV = 0, 32, 64, 96, 128
PIECES = {"v1": (LV + 16, LV + 32), "s1": (LS + 16, LV + 16), "r1": (LS + 8, LS + 16), "r0": (LA, LS + 8)}
SCRATCH = {k: ("psum", [128, 512], F32) for k in ("psR0", "psR1", "psS0", "psS1", "psA0", "psA1", "psL", "psH")}
for _d, _s in [
    (BF, "xin 2048 X1 2048 X2 2048 uin 512 vin 512 P 2048 dw 2112 ones 516 ce 516 cc 2048 gm 128 c16 128 t16 256 sg 1024 A 512 Lx 32 "
         "E 2304 cs 2304 eye 32 s8 128 mk 576 FA 512 FB 512 ra 512 rb 512 pp 768"),
    (MX, "uq 128 vq 128 wq 512 kq 512 eq 512 xq_0 512 xq_1 512 xq_2 512 sq 256 pq_0 512 pq_1 512 lc_0 512 lc_1 512"),
    (U8, "us 128 vs 128 wsc 512 ks 512 es 512 xs_0 512 xs_1 512 xs_2 512 ss 256 psc_0 512 psc_1 512 ls_0 512 ls_1 512"),
    (F32, "yo 512 p64 1 pF 5 col 17 t8 128 k8 128 kH 128 cp0 32 cp 32 c0 16 cA 16 cB 16 cN 16 sy 256 sh 256 win 512 vv 512 tab_0 1152 tab_1 1152 "
          "m0 64 e0 64 o0 64 m1 96 e1 96 o1 96 m2 128 e2 128 o2 128 ps 512 FG 1024 sn 1024 rr 64"),
    (I32, "pI 1 pK 5 n1 32 ii 32"),
    (U16, "ends 4 lq_0 160 lq_1 160 ql_0 160 ql_1 160 of2 32 li_0 32 li_1 32"),
]:
    _s = _s.split()
    for _i in range(0, len(_s), 2):
        SCRATCH[_s[_i]] = ("sbuf", [128, int(_s[_i + 1])], _d)
SEMAPHORES = ["sv", "sa", "sp", "sg", "ldx0", "ldx1", "ldu", "ldv", "ldw", "ldws", "ldm", "sty0", "sty1", "sty2", "stc0", "stc1", "stc2", "sts", "sent"]
SEMAPHORES += ["got%s%d" % (_k, _t) for _k in ("c0", "c1", *PIECES) for _t in range(ROUNDS)]


def rank_program(g, core, T, topo):
    me = T.rank_of(core)
    if me is None:
        return
    n = len(T.cores)
    nxt, prv = T.cores[(me + 1) % n], T.cores[(me - 1) % n]
    V, S, PE = g.vector, g.scalar, g.tensor
    queue = {"v": V, "a": S, "p": PE, "g": g, "y": g.sync}
    own = {"v": "sv", "a": "sa", "p": "sp", "g": "sg"}
    count = {"sv": 0, "sa": 0, "sp": 0, "sg": 0}
    seen = {q: {} for q in queue}
    sent = [0]
    c = {}
    st = {}

    def need(q, deps):
        for d in deps:
            if d is not None and seen[q].get(d[0], 0) < d[1]:
                queue[q].wait_ge(T.sem[d[0]], d[1])
                seen[q][d[0]] = d[1]

    def done(q, ins):
        s = own[q]
        ins.then_inc(T.sem[s], 1)
        count[s] += 1
        return (s, count[s])

    def vec(deps, fn, *a):
        need("v", deps)
        return done("v", fn(*a))

    def ts(deps, out, in0, s1, s2, *ops):
        return vec(deps, V.tensor_scalar, out, in0, s1, s2, *ops)

    def tt(deps, out, in0, in1, op):
        return vec(deps, V.tensor_tensor, out, in0, in1, op)

    def fill(deps, out, value):
        return vec(deps, V.memset, out, value)

    def copy(deps, out, in_):
        return vec(deps, V.tensor_copy, out, in_)

    def quant(deps, q, s, in_):
        return vec(deps, V.quantize_mx, q, s, in_)

    def pick(deps, out, data, push, low):
        return vec(deps, V.tensor_tensor_scan, out, data, push, low, OP.max, OP.add)

    def chain(deps, out, factor, term):
        return vec(deps, V.tensor_tensor_scan, out, factor, term, 0.0, OP.mult, OP.add)

    def act(deps, out, in_, func=AF.Copy, **kw):
        need("a", deps)
        return done("a", S.activation(out, in_, func, **kw))

    def mm(deps, out, lq, ls, rq, rs):
        need("p", deps)
        return done("p", PE.matmul_mx(out, lq, ls, rq, rs, True, True))

    def iota(out, pattern, base=0, cm=0):
        return done("g", g.iota(out, pattern, base, cm, allow_small_or_imprecise_dtypes=True))

    def dma(q, sem, out, in_, deps=()):
        need(q, deps)
        queue[q].dma_start(out, in_).then_inc(T.sem[sem], 16)
        return (sem, 16)

    def remote(deps, out, in_, sem):
        need("g", deps)
        rid, pid = topo.addr(prv)[:2]
        g.remote_dma(out, in_, T.sem[sem], T.sem.sent, pid, rid, topo.mask(core, prv))
        sent[0] += len(topo.engines(core, prv))

    def cut(h, w):
        return slice(w * h, w * h + w)

    ein = len(topo.engines(nxt, core))
    psR, psS, psA = (T.psR0, T.psR1), (T.psS0, T.psS1), (T.psA0, T.psA1)
    col = lambda j: T.col[:, j:j + 1]
    pF = lambda j: T.pF[:, j:j + 1]

    d_x = {HI: dma("y", "ldx1", T.xin[:, 1024:2048], T.x[:, 1024:2048])}
    d_u = dma("a", "ldu", T.uin[:], T.u[:])
    d_x[LO] = dma("y", "ldx0", T.xin[:, 0:1024], T.x[:, 0:1024])
    d_w = dma("y", "ldw", T.wq[:].bitcast(dt.uint8), T.wc[:])
    d_ws = dma("y", "ldws", T.wsc[:], T.ws[:])
    d_v = dma("y", "ldv", T.vin[:], T.v[:])

    c["p64"] = iota(T.p64[:], [[0, 1]], -64, 1)
    c["pI"] = done("g", g.iota(T.pI[:], [[0, 1]], 0, 1))
    c["c16"] = iota(T.c16[:], [[1, 8], [0, 16]])
    c["cp0"] = iota(T.cp0[:], [[0, 4], [16, 8]])
    c["t8"] = iota(T.t8[:], [[0, 16], [1, 8]])
    c["win"] = iota(T.win[:], [[1, 512]])
    c["m0"] = iota(T.m0[:], [[0, 64]])
    tabs = [iota(T.tab_0[:, 0:1024], [[0, 1024]])]
    c["ones"] = iota(T.ones[:], [[0, 516]], 1)

    t_b = fill([], col(0), 63.0 * LN2)
    t_eb = fill([], col(1), BL / 64.0)
    fill([], T.cc[:, 0:512], 0.0)
    for j, (sh, am) in enumerate([(0, 15), (4, 7), (1, 7), (0, 7), (3, 1)]):
        z = ts([c["pI"]], T.pK[:, j:j + 1], T.pI[:], sh, am, OP.logical_shift_right, OP.bitwise_and)
    fill([], T.cc[:, 512:1024], 0.0)
    t_pF = copy([z], T.pF[:], T.pK[:])
    act([c["p64"]], col(2), T.p64[:], AF.Exp, scale=LN2)
    t_w = act([t_pF, t_b], col(16), pF(1), AF.Exp, bias=col(0), scale=-16.0 * LN2)
    t_cz = fill([], T.cc[:, 1024:2048], 0.0)
    ts([t_pF], col(3), pF(0), 10.0, -1.0, OP.is_lt, OP.mult)
    z = ts([], col(4), pF(0), 10.0, -2.0 ** -10, OP.is_ge, OP.mult)
    t_gm = ts([c["c16"]], T.gm[:], T.c16[:], pF(1), None, OP.is_equal)
    t_cp = ts([c["cp0"]], T.cp[:], T.cp0[:], pF(0), None, OP.add)
    z = ts([z], col(5), pF(0), 12.0, col(4), OP.is_lt, OP.mult)
    ts([t_w, z], col(10), col(2), col(16), col(3), OP.mult, OP.mult)
    t_wh = ts([], col(11), col(2), col(16), col(5), OP.mult, OP.mult)
    q_u = quant([d_u], T.uq[:], T.us[:], T.uin[:])
    z = act([], col(6), pF(2), scale=-1.0, bias=0.5)
    act([], col(9), pF(2), scale=BL, bias=-8.0 * BL)
    z = act([z, c["t8"]], T.s8[:], T.t8[:], AF.Sign, bias=col(6))
    c["c0"] = act([t_cp], T.c0[:], T.cp[:, 0:16], scale=-1.0, bias=BL + 511.5 - 1024.0)
    for kk in (T.k8, T.kH):
        c["k8"] = act([z], kk[:], T.s8[:], scale=BL)
    act([c["win"]], T.sg[:, 513::2], T.win[:, 0:256], scale=0.0)
    for at, step, w in ((0, 4, 10), (514, 4, 10), (1024, 8, 10), (1030, 8, 10), (1536, 8, 11), (1542, 8, 11)):
        top = at // 512 * 512 + 512
        src = T.gm[:] if step == 4 else T.gm[:, at % 8 // 6::2]
        t_cc = ts([t_wh, t_gm, t_cz], T.cc[:, at:top:step], src, col(w), None, OP.mult)

    def constants_1():
        act([], T.sg[:, 1:512:2], T.win[:, 0:256], scale=0.0)
        act([], col(12), pF(3), scale=160.0, bias=15.0)
        c["e"] = act([], col(13), pF(3), scale=-144.0, bias=1151.0)
        c["e0"] = act([], T.e0[:, 1::2], T.cp[:], bias=1024.0)
        c["k"] = quant([t_cc], T.kq[:], T.ks[:], T.cc[:])

    def factors_1():
        z = ts([c["win"]], T.eye[:, 16:32], T.win[:, 0:16], pF(0), 255.0, OP.is_equal, OP.mult)
        fill([], T.mk[:], 1.0)
        c["mk"] = ts([z], T.eye[:, 0:16], T.eye[:, 16:32], 1.0, None, OP.add)

    def factors_2():
        fill([c["mk"]], T.mk[:, 144:576:144], 0.0)
        z = fill([], T.mk[:, 16:576:160], 0.0)
        for s in range(8):
            a = SEG[s] + 16 * s
            dma("y", "ldm", T.mk[:, a:a + 16], T.eye[:, 0:16], [z])
        ts([c["k8"]], T.k8[:, 7::8], T.cp[:, 0:16], 0.0, col(9), OP.mult, OP.add)
        c["k8"] = ts([], T.kH[:, 7::8], T.cp[:, 0:16], 4.0, col(9), OP.mult, OP.add)
        c["e"] = ts([c["e"]], col(12), col(12), col(13), None, OP.min)

    def ends():
        z = ts([c["e"]], col(13), pF(4), 576.0, col(12), OP.mult, OP.add)
        copy([], T.ends[:, 2:3], col(12))
        own_h(HI)
        for h in range(2):
            c["ends"] = ts([z], T.ends[:, h:h + 1], col(13), 1152.0 * h, None, OP.add)

    def pushes():
        z = act([], col(8), pF(0), scale=-1.0, bias=0.5)
        act([], col(14), pF(0), bias=-16.0)
        for j in (2, 1, 0):
            c["pp", j] = act([z, c["t16"]], T.pp[:, cut(j, 256)], T.t16[:], AF.Sign, bias=col(8))
        for h in range(2):
            c["ps"] = act([c["pp", 2]], T.ps[:, cut(h, 256)], T.pp[:, 512:768], scale=BS)

    def terms():
        act([], T.e1[:, 1::3], T.cp[:], scale=-1.0, bias=-1024.0)
        c["e1"] = act([], T.e1[:, 2::3], T.cp[:], bias=1024.0)
        act([], T.cA[:], T.cp[:, 0:16], bias=BS - 512.0)
        act([], T.cB[:], T.cp[:, 0:16], bias=BS)
        c["terms"] = act([], T.cN[:], T.cp[:, 0:16], scale=-1.0, bias=-BS)

    def patterns():
        iota(T.m1[:], [[0, 32], [1, 3]])
        iota(T.m2[:], [[0, 32], [1, 2], [0, 2]])
        c["later"] = iota(T.e2[:], [[0, 128]], 512)

    def unpackers():
        need("g", [c["ones"]])
        c["ce"] = done("g", g.affine_select(T.ce[:], T.ones[:], [[-1, 516]], OP.is_equal, 0.0, 3, 4))

    def unpacker(b):
        c["eq", b] = quant([c["ce"]], T.eq[:, cut(b, 128)], T.es[:, cut(b, 128)], T.ce[:, 3 - b:515 - b])

    def k(i):
        return T.kq[:, cut(i, 128)], T.ks[:, cut(i, 128)]

    def own_a(h):
        st["sy", h] = st["freeL"] = pick([st["L"], c["k8"]], T.sy[:, cut(h, 128)], T.psL[:, 0:128], T.k8[:], -2.0 * BL)

    def own_h(h):
        st["sh", h] = st["freeH"] = pick([st["H"]], T.sh[:, cut(h, 128)], T.psH[:, 0:128], T.kH[:], -2.0 * BL)

    rest = []

    for t in range(ROUNDS + 1):
        B = lambda name, t=t: T["%s_%d" % (name, t)]
        xq, xs, P = B("xq"), B("xs"), T.P
        X = T.xin if t == 0 else T["X%d" % t]

        def add(b, a, e):
            w = slice(4 * a + b, 4 * e, 4)
            st["x"] = tt([st["li", a // 256], st["dw", b]], X[:, w], T.dw[:, 528 * b:528 * b + 513].indirect(T["li_%d" % (t - 1)][:, a // 16:e // 16]), P[:, w], OP.add)
            if rest and b in (0, 3 if t < ROUNDS else 1):
                rest.pop(0)()

        def state(a, e):
            st["q", a // 256] = quant([d_x[a // 256] if t == 0 else st["x"]], xq[:, a:e], xs[:, a:e], X[:, 4 * a:4 * e])
            return st["q", a // 256]

        if t == ROUNDS:
            parts = ((256, 512, T.psS1), (128, 256, T.psS0), (0, 128, T.psA0))
            add(0, 256, 512)
            for j, (a, e, ps) in enumerate(parts):
                for b in range(1, 4):
                    add(b, a, e)
                if j == 2:
                    dma("a", "sty1", T.y[:, 128:256], T.yo[:, 128:256], [y])
                else:
                    z = st["x"]
                    add(0, *parts[j + 1][:2])
                    st["x"] = z
                q = state(a, e)
                y = mm([q, c["vq"]], ps[:, 0:e - a], T.vq[:], T.vs[:], xq[:, a:e], xs[:, a:e])
                dma("y", "stc%d" % j, T.oc[:, 4 * a:4 * e], xq[:, a:e].bitcast(dt.uint8), [q])
                if j < 2:
                    y = act([y], T.yo[:, a:e], ps[:, 0:e - a])
                    if j == 0:
                        dma("a", "sty0", T.y[:, a:e], T.yo[:, a:e], [y])
                else:
                    need("a", [q])
                    for i in range(4):
                        S.dma_start(T.osc[4 * i:4 * i + 4, :], xs[32 * i:32 * i + 4, :]).then_inc(T.sem.sts, 16)
                    y = copy([y], T.yo[:, a:e], ps[:, 0:e - a])
                    dma("y", "sty2", T.y[:, a:e], T.yo[:, a:e], [y])
            break
        tab, lq, ql = B("tab"), B("lq"), B("ql")

        def send(name, deps):
            w = slice(*PIECES[name])
            remote(deps, ql[:, w], lq[:, w], "got%s%d" % (name, t))

        def got(name):
            return ("got%s%d" % (name, t), ein)

        def scores(h):
            st["s", h] = mm([st["q", h], q_u], psS[h][:, 0:256], T.uq[:], T.us[:], xq[:, cut(h, 256)], xs[:, cut(h, 256)])

        def signs(h):
            st["sg", h] = st["free", psS[h].name] = act([st["s", h]], T.sg[:, 512 * h:512 * h + 512:2], psS[h][:, 0:256], AF.Sign, bias=7.7e-34)

        def layer(h, b):
            ps = ((T.psR1, T.psS0, T.psS1, T.psR0), (T.psR0, T.psR1, T.psS1, T.psR0))[h][b]
            r = mm([d_w, d_ws, st["q", h], st.get(("free", ps.name))], ps[:, 0:256], T.wq[:, cut(b, 128)], T.wsc[:, cut(b, 128)], xq[:, cut(h, 256)], xs[:, cut(h, 256)])
            st["P", h] = st["free", ps.name] = act([r], P[:, 1024 * h + b:1024 * h + 1024:4], ps[:, 0:256], scale=0.03125)

        def keys(h):
            q = quant([st["sg", h]], T.sq[:, cut(h, 128)], T.ss[:, cut(h, 128)], T.sg[:, cut(h, 512)])
            for name, out, i in (("A0", T.psA0, 0), ("L", T.psL, 2), ("A1", T.psA1, 1), ("H", T.psH, 3)):
                st[name] = mm([q, c["k"], st.get("free" + name)], out[:, 0:128], *k(i), T.sq[:, cut(h, 128)], T.ss[:, cut(h, 128)])

        def spread(h):
            for e in range(2):
                st["A", h] = st["freeA%d" % e] = act([st["A%d" % e]], T.A[:, 256 * h + e:256 * h + 256:2], psA[e][:, 0:128], AF.Exp, scale=1.0 / 64.0)

        def spread_own(h):
            st["Lx", h] = act([st["sy", h], t_eb], T.Lx[:, cut(h, 16)], T.sy[:, 128 * h + 7:128 * h + 128:8], AF.Exp, bias=col(1), scale=1.0 / 64.0)

        def lists(h):
            st["e0", h] = tt([c["c0"], st["sy", h]], T.e0[:, 32 * h:32 * h + 32:2], T.sy[:, 128 * h + 7:128 * h + 128:8], T.c0[:], OP.add)
            st["lv", h] = ts([st["sh", h]], lq[:, LV + 16 * h:LV + 16 * h + 16], T.sh[:, 128 * h + 7:128 * h + 128:8], BL + 1.5, None, OP.add)

        def entry(r):
            st["vv", r] = act([got("v1" if r > 1 else "s1"), c["win"]], T.vv[:, cut(r, 128)], T.win[:].indirect(ql[:, LV + 8 * r:LV + 8 * r + 8]), scale=0.25, bias=128.0 * r + 0.125)

        def equal(r, blocks=range(8)):
            for s in blocks:
                a = 576 * r + SEG[s]
                st["E", r] = ts([st["A", r // 2], st["Lx", r // 2]], T.E[:, a:a + 16 * s + 16], T.A[:, 128 * r:128 * r + 16 * s + 16], T.Lx[:, 8 * r + s:8 * r + s + 1], None, OP.is_equal)

        def earlier(r):
            st["cs", r] = chain([st["E", r], ("ldm", 128)], T.cs[:, cut(r, 576)], T.mk[:], T.E[:, cut(r, 576)])

        def first(r, w, deps):
            e = 0 if w == 2 else 2
            return ts([st["cs", r], c["ends"], c["m0"], *deps], T.m0[:, 16 * r + 1:16 * r + 32:2], T.cs[:, 576 * r:576 * (r + w)].indirect(T.ends[:, e:e + 1]), 128.0, None, OP.is_lt)

        def slot(r, w, deps):
            a = slice(16 * r, 16 * (r + w))
            return chain(deps, T.o0[:, a], T.m0[:, a], T.e0[:, a])

        def offsets(r, w, dep):
            return copy([dep], lq[:, LS + 8 * r:LS + 8 * (r + w)], T.o0[:, 16 * r + 1:16 * (r + w):2])

        def scatter(r, of, *deps):
            st["sc"] = copy([st["vv", r], *deps], tab[:, 0:1152].indirect(of), T.vv[:, cut(r, 128)])

        def pack_p(r):
            st["pq"] = quant([st["P", r // 2]], B("pq")[:, cut(r, 128)], B("psc")[:, cut(r, 128)], P[:, cut(r, 512)])

        def send_p(h):
            remote([st["pq"]], B("lc")[:, cut(h, 256)].bitcast(dt.uint8), B("pq")[:, cut(h, 256)].bitcast(dt.uint8), "gotc%d%d" % (h, t))
            remote([], B("ls")[:, cut(h, 256)], B("psc")[:, cut(h, 256)], "gotc%d%d" % (h, t))

        def unpack(h):
            for b, ps in enumerate(psR + psA):
                D = mm([c["eq", b], ("gotc%d%d" % (h, t), 2 * ein), st["pq"], st.get(("dw", b))], ps[:, 0:256], T.eq[:, cut(b, 128)], T.es[:, cut(b, 128)],
                       B("lc")[:, cut(h, 256)], B("ls")[:, cut(h, 256)])
                st["dw", b] = act([D], T.dw[:, 528 * b + 256 * h:528 * b + 256 * h + 256], ps[:, 0:256])
            st["freeA0"] = st["freeA1"] = st["dw", 3]

        if t > 0:
            for b in range(4):
                add(b, 256, 512)
        state(256, 512)
        scores(HI)
        signs(HI)
        if t == 0:
            constants_1()
            state(0, 256)
            factors_1()
        else:
            layer(HI, 0)
            layer(HI, 1)
            for b in range(3):
                add(b, 0, 256)
        keys(HI)
        spread(HI)
        if t > 0:
            add(3, 0, 256)
            own_a(HI)
            state(0, 256)
            own_h(HI)
        else:
            factors_2()
            own_a(HI)
            ends()
        scores(LO)
        spread_own(HI)
        signs(LO)
        for b in range(3) if t == 0 else (2, 3):
            layer(HI, b)
        lists(HI)
        send("v1", [st["lv", HI]])
        if t == 0:
            c["t16"] = iota(T.t16[:], [[0, 16], [1, 16]])
        equal(3)
        equal(2, range(2))
        keys(LO)
        spread(LO)
        equal(2, range(2, 8))
        earlier(3)
        own_a(LO)
        spread_own(LO)
        if t == 0:
            layer(HI, 3)
        earlier(2)
        own_h(LO)
        z = first(2, 2, [])
        lists(LO)
        equal(1, range(1))
        z = slot(2, 2, [z, c["e0"]])
        for b in range(4):
            layer(LO, b)
        entry(3)
        entry(2)
        equal(1, range(1, 4))
        z = offsets(2, 2, z)
        send("s1", [z])
        if t == 0:
            unpackers()
        equal(1, range(4, 8))
        equal(0, range(3))
        earlier(1)
        equal(0, range(3, 6))
        z = first(1, 1, [])
        equal(0, range(6, 8))
        z2 = ts([], T.n1[:], T.sy[:, 7::8], BL + 512.5, None, OP.add)
        z = z1 = slot(1, 1, [z])
        ts([], lq[:, LA:LA + 32], T.sy[:, 7::8], BL + 511.5, None, OP.add)
        earlier(0)
        z = offsets(1, 1, z)
        send("r1", [z])
        entry(1)
        entry(0)
        z2 = ts([z2], T.ii[:], T.n1[:], 1023, None, OP.bitwise_and)
        if t == 0:
            pushes()
            fill([], T.FA[:, 0:128], 0.5)
        z = first(0, 1, [z1])
        ts([], lq[:, LC:LC + 32], T.cs[:].indirect(T.ends[:, 0:2]), 1.0 / 256.0, None, OP.mult)
        copy([z2], lq[:, LB:LB + 32], T.ii[:])
        z = slot(0, 1, [z])
        pack_p(3)
        z = offsets(0, 1, z)
        send("r0", [z])
        scatter(3, ql[:, LS + 24:LS + 32], tabs[t], got("s1"))
        pack_p(2)
        send_p(HI)
        if t == 0:
            patterns()
        scatter(2, ql[:, LS + 16:LS + 24], st["sc"])
        pack_p(1)
        if t == 0:
            unpacker(0)
            unpacker(1)
        scatter(1, ql[:, LS + 8:LS + 16], st["sc"], got("r1"))
        pack_p(0)
        send_p(LO)
        if t == 0:
            tabs.append(iota(T.tab_1[:, 0:1024], [[0, 1024]]))
        scatter(0, ql[:, LS:LS + 8], st["sc"], got("r0"))
        pa = ts([c["pp", 0]], T.pp[:, 15:512:16], ql[:, LC:LC + 32], -0.5, col(14), OP.mult, OP.add)
        e1 = copy([c["later"]], T.e1[:, 0::3], ql[:, LB:LB + 32])
        if t == 0:
            ts([], col(15), col(14), BS, -0.125, OP.mult, OP.add)
        win = tab[:, 0:1024]
        fb = {h: act([st["sc"]], T.FB[:, cut(h, 256)], win.indirect(ql[:, LB + 16 * h:LB + 16 * h + 16]), AF.Sign) for h in (HI, LO)}
        if t == 0:
            terms()

        def inside(r):
            return ts([st["sc"]], T.FA[:, cut(r, 128)], win.indirect(ql[:, LA + 8 * r:LA + 8 * r + 8]), 128.0 * r, 0.5, OP.is_ge, OP.mult)

        def second(h, z):
            pick([z, pa], T.ra[:, cut(h, 256)], T.FA[:, cut(h, 256)], T.pp[:, cut(h, 256)], -4.0)
            yield
            z = pick([fb[h], c["pb"]], T.rb[:, cut(h, 256)], T.FB[:, cut(h, 256)], T.pp[:, 512:768], -4.0)
            yield
            w = slice(256 * h + 15, 256 * h + 256, 16)
            z = tt([z], T.m1[:, 48 * h + 2:48 * h + 48:3], T.ra[:, w], T.rb[:, w], OP.is_equal)
            yield
            z = chain([z, e1, c["e1"]], T.o1[:, cut(h, 48)], T.m1[:, cut(h, 48)], T.e1[:, cut(h, 48)])
            yield
            st["of", h] = copy([z], T.of2[:, cut(h, 16)], T.o1[:, 48 * h + 2:48 * h + 48:3])
            yield

        inside(3)
        z = inside(2)
        if t == 0:
            c["pb"] = ts([c["ps"]], T.pp[:, 527::16], T.cp[:, 0:16], 0.0, col(14), OP.mult, OP.add)
        both = {HI: second(HI, z), LO: second(LO, inside(1))}
        for h in (HI, HI, LO, HI, LO, HI, LO, HI, LO):
            next(both[h])
        for r in (3, 2, 1, 0):
            scatter(r, T.of2[:, cut(r, 8)], st["sc"], fb[LO], st["of", r // 2])
            if r == 3:
                next(both[LO])
                if t == 0:
                    unpacker(2)
                    unpacker(3)
                unpack(HI)
            if r == 2:
                f_b = ts([], T.ps[:, 15::16], lq[:, LV:LV + 32], -0.25, col(15), OP.mult, OP.add)
            if t == 0 and r == 2:
                fill([], T.dw[:, 512:2112:528], 0.0)
            if t == 0 and r == 1:
                c["vq"] = quant([d_v], T.vq[:], T.vs[:], T.vin[:])
        fg = {}
        for h in (HI, LO):
            for look in range(2):
                a = LA + 32 * look + 16 * h
                fg[h, look] = (copy if (h, look) == (HI, 0) else act)([st["sc"]], T.FG[:, cut(2 * h + look, 256)], win.indirect(lq[:, a:a + 16]))
        unpack(LO)

        def search(h, B=B, fg=fg, f_b=f_b):
            for look in range(2):
                z = pick([fg[h, look], f_b], T.sn[:, cut(2 * h + look, 256)], T.FG[:, cut(2 * h + look, 256)], T.ps[:, cut(h, 256)], -2.0 * BS)
                yield
            r0, r1 = (T.sn[:, 512 * h + 256 * look + 15:512 * h + 256 * look + 256:16] for look in range(2))
            z = ts([z], T.rr[:, cut(h, 32)], T.sn[:, 512 * h + 15:512 * h + 512:16], ROUNDER, -ROUNDER, OP.add, OP.add)
            tt([c["terms"]], T.e2[:, 64 * h:64 * h + 64:4], r1, T.cA[:], OP.add)
            tt([], T.e2[:, 64 * h + 2:64 * h + 64:4], T.cN[:], r0, OP.subtract)
            tt([], T.e2[:, 64 * h + 3:64 * h + 64:4], r0, T.cB[:], OP.add)
            yield
            tt([z], T.m2[:, 64 * h + 1:64 * h + 64:4], r1, T.rr[:, 32 * h + 16:32 * h + 32], OP.is_equal)
            z = tt([], T.m2[:, 64 * h + 3:64 * h + 64:4], r0, T.rr[:, 32 * h:32 * h + 16], OP.not_equal)
            yield
            z = chain([z], T.o2[:, cut(h, 64)], T.m2[:, cut(h, 64)], T.e2[:, cut(h, 64)])
            yield
            st["li", h] = copy([z], B("li")[:, cut(h, 16)], T.o2[:, 64 * h + 3:64 * h + 64:4])
            yield

        both = {h: search(h) for h in (HI, LO)}
        for h in (HI, HI, LO, HI, HI, LO, HI, LO, HI, LO):
            next(both[h])
        rest += [lambda s=both[LO]: next(s)] * 2

    need("g", [(s, n) for s, n in count.items()])
    g.wait_ge(T.sem.sent, sent[0])
    need("y", [("stc0", 16), ("stc1", 16), ("stc2", 16), ("sty2", 16)])
    need("a", [("sty0", 16), ("sty1", 16), ("sts", 64)])
